import numpy as np, ml_dtypes
CORES = [66,74,82,90,194,202,210,218]
N = 8
BF = ml_dtypes.bfloat16
W, K, P, RO, LIM = 4096, 8, 256, 6, 88
def hashed(u, v):
    u = u & 4095; v = v & 4095
    return ((u * v >> 5) + 37 * u) & (W - 1)
def probe(w, v):
    s = np.matmul(w, v.astype(np.float32)).astype(np.int64)
    return hashed(s[:, :, 0], s[:, :, 1])
def masks(rng, size):
    o = np.argsort(np.argsort(rng.random((N, 8, 16, K)), axis=2), axis=2)
    return (o < size[:, :, None, :]).astype(np.int32)
def parts(rng):
    x = rng.integers(0, 256, (N, 8, 16, W), dtype=np.uint8).astype(np.int32)
    return x, masks(rng, rng.integers(4, 12, (N, 8, K))), rng.integers(0, 256, (N, 8, 16, P)), rng.integers(0, 256, (N, 8, 16, 2))
def pack(x, m, z, w):
    return {a: np.ascontiguousarray(v.reshape(N, 128, n)).astype(np.float32).astype(BF) for a, v, n in (("xr", x, W), ("m0", m, K), ("z0", z, P), ("wt", w, 2))}
def setup_inputs(rng):
    return pack(*parts(rng))
def setup_inputs_spread(rng):
    def uneven(n):
        v = (np.exp2(8 * rng.random((N, 8, 1, n))) * rng.random((N, 8, 16, n))).astype(np.int32)
        return np.where(rng.random((N, 8, 1, n)) < 0.5, v, 255 - v)
    lo = rng.choice(np.array([0, 2, 5]), (N, 8, 1))
    return pack(uneven(W), masks(rng, lo + ((17 - lo) * rng.random((N, 8, K))).astype(np.int64)), uneven(P), np.exp2(8 * rng.random((N, 8, 16, 2))).astype(np.int64))
def setup_inputs_ends(rng):
    def two(n): return 255 * rng.integers(0, 2, (N, 8, 16, n), dtype=np.int32)
    x, z, w = two(W), two(P), two(2); m = rng.integers(0, 2, (N, 8, 16, K))
    s = 255 * rng.integers(0, 2, (8, 8, 1)); s[7] = 255
    z[N - 1, :, :8] = s; x[N - 1, :, :8] = 255 - s
    z[1, 7, :8] = 255; x[1, 7, :8] = 0
    for q, g in [(N - 1, g) for g in range(8)] + [(1, 7)]:
        a = rng.integers(0, 8, K); b = (a + rng.integers(1, 8, K)) % 8
        m[q, g, a, np.arange(K)] = 1; m[q, g, b, np.arange(K)] = 1
    m[1, 7, :, K - 1] = 0; m[1, 7, 15, K - 1] = 1
    w[N - 1, 7] = 255; m[N - 1, 7, :, 0] = 1; m[N - 1, 7, :, K - 1] = 1
    for i in (0, 1, 6, P - 1): z[N - 1, 7, :, i] = 255
    x[N - 1, 7, :, int(hashed(16 * 255 * 255, 16 * 255 * 255))] = 0
    for i in (0, 3, P - 1): z[0, 7, :, i] = 0
    x[0, 7, :, 0] = 0; m[0, 6, :, K - 1] = 0
    for g, e in ((7, 0), (5, 1)):
        w[2, g, :, e] = 255; w[2, g, :, 1 - e] = 255 * (rng.permutation(16) < rng.integers(1, 16))
        m[2, g, :, 0] = 1; x[2, g, 0] = 0
        for i in (0, 3, P - 1): z[2, g, :, i] = 255
        x[2, g, :, int(hashed(255 * int(np.sum(w[2, g, :, 0])), 255 * int(np.sum(w[2, g, :, 1]))))] = 255
    x[2, 6, 14:16] = 0; z[2, 6, 14:16, :8] = 255
    m[2, 6, :, 0] = 0; m[2, 6, 14] = 0; m[2, 6, 14:16, 0] = 1
    return pack(x, m, z, w)
def setup_inputs_corners(rng):
    x, m, z, w = parts(rng); idx = np.concatenate([np.arange(0, P, 2), np.array([P - 1])])
    t = np.argwhere(hashed(np.arange(256)[:, None], np.arange(256)[None, :]) == W - 1)
    for q in range(N):
        order = rng.permutation(8)
        want = {0: 0, 1: 7, N - 2: 0, N - 1: 4}.get(q)
        if want is not None:
            i = int(np.argmax(order == want)); order[i] = order[7]; order[7] = want
        for g in range(8):
            a, b, c, e = x[q, g], m[q, g], z[q, g], w[q, g]; kind = int(order[g])
            if kind == 0: b[:, 0] = 0
            if kind == 1: b[:] = 1
            if kind == 2:
                b[:] = 1; b[:, K - 1] = 0; b[15, K - 1] = 1
            if kind == 3:
                a[:] = rng.integers(250, 256, a.shape); c[:] = rng.integers(0, 6, c.shape)
                b[:] = np.argsort(np.argsort(rng.random((16, K)), axis=0), axis=0) < rng.integers(2, 4, (1, K))
            if kind == 4:
                e[:] = 0; e[0, 0] = 1; e[1, 1] = 1; b[0:2] = 1
                p = t[rng.integers(0, len(t), len(idx))]; c[0, idx] = p[:, 0]; c[1, idx] = p[:, 1]; c[0, 1] = 0
            if kind == 5:
                e[:] = 0; e[0] = 15; e[1] = 27; b[0:2] = 1; c[0, idx] = 255; c[1, idx] = 10
            if kind == 6:
                a[:] = 128; c[:] = 128 + rng.choice(np.array([-LIM - 1, -LIM, LIM, LIM + 1]), c.shape)
    p = t[rng.integers(0, len(t))]; odd = np.arange(2 * int(rng.integers(0, P // 4)) + 1, P, 2)
    m[N - 1, 7, :, 0] = 0; m[N - 1, 7, 0:2, 0] = 1; x[N - 1, 7, 0:2, W - 1] = p
    z[N - 1, 7, 0] = 0; z[N - 1, 7, 0, odd] = p[0]; z[N - 1, 7, 1, odd] = p[1]
    z[N - 2, 7, 0] = p[0]; z[N - 2, 7, 1] = p[1]; x[N - 2, 7, :, 0] = 0
    o = rng.permutation(256)[:P]
    w[1, 7] = 0; w[1, 7, 0, 0] = 1; m[1, 7, :, 0] = 0; m[1, 7, 0, 0] = 1; z[1, 7, 0] = o
    z[0, 7, 0] = o[P - 1]; x[0, 7, :, 0] = 0
    return pack(x, m, z, w)
def setup_inputs_crowd(rng):
    x, m, z, w = parts(rng); role = rng.permutation(N)
    for q in range(N):
        r = int(role[q]); k = rng.permutation(8)
        if r == 1: k = np.roll(k, 4 - int(np.argmax(k == rng.integers(3, 5))))
        if r < 3: x[q] = rng.integers(200, 256, (8, 16, W))
        if r < 2: z[q] = rng.integers(0, 101, (8, 16, P))
        if r == 2: z[q] = rng.integers(200, 256, (8, 16, P))
        w[q, k[0]] = 0; w[q, k[1]] = 0
        for g in k[2:4]:
            w[q, g] = 0; w[q, g, 0] = 1; m[q, g, 0] = 1
            c = int(rng.integers(0, 100)) if r < 2 else int(rng.integers(200, 255))
            z[q, g, 0] = c; z[q, g, 0, int(rng.integers(0, P))] = c + 1
        if r == 1: z[q, k[4], :, int(rng.integers(0, P))] = 210
        if r == 2: z[q, k[4], :, int(rng.integers(0, P))] = 50
    return pack(x, m, z, w)
def check_inputs(d):
    bad = []
    for k, lo, hi in (("xr", 0, 255), ("m0", 0, 1), ("z0", 0, 255), ("wt", 0, 255)):
        a = np.asarray(d[k]).astype(np.float32)
        if not (np.min(a) >= lo and np.max(a) <= hi): bad.append("range of " + k)
        elif np.any(a != np.floor(a)): bad.append("whole numbers in " + k)
    return bad
def reference(xr, m0, z0, wt):
    X = xr.astype(np.float32).astype(np.int16).reshape(N, 8, 16, W)
    M = np.repeat(m0.astype(np.float32).astype(np.int16).reshape(N, 8, 16, K)[..., None], P, axis=4)
    z = z0.astype(np.float32).astype(np.int16).reshape(N, 8, 16, P)
    w = np.ascontiguousarray(wt.astype(np.float32).reshape(N, 8, 16, 2).transpose(0, 1, 3, 2))
    A = np.zeros(N, np.int64); kk = np.arange(K)[None, None, :, None]; steps = []
    for t in range(RO):
        zk = z[:, :, :, None, :]
        h = probe(w, (M * zk).reshape(N, 8, 16, K * P))
        Xh = np.take_along_axis(X, h[:, :, None, :], 3).reshape(N, 8, 16, K, P)
        F = M * (np.abs(Xh - zk) > LIM)
        ok = np.add.reduce(F, axis=2, dtype=np.int16) <= (1 + (A & 1))[:, None, None, None]
        j = np.where(np.any(ok, axis=2), np.argmax(ok, axis=2), K)
        first = F * (np.add.accumulate(F, axis=2, dtype=np.int16) == 1)
        U = np.max(first * (kk < j[:, :, None, :])[:, :, None], axis=3)
        hit = (j < K)[:, :, None, :]; s = np.where(j < K, j, 0)[:, :, None, None, :]
        U = np.maximum(U, hit * np.take_along_axis(M, s, 3)[:, :, :, 0])
        xs = np.take_along_axis(Xh, s, 3)[:, :, :, 0]
        new = np.where(hit, np.abs(z - xs), (z + xs) >> 1)
        down = (kk[:, :, 1:] <= j[:, :, None, :])[:, :, None]
        M = np.concatenate([U[:, :, :, None], np.where(down, M[:, :, :, :-1], M[:, :, :, 1:])], axis=3)
        if t < RO - 1:
            place = probe(w, U * z)
            for q in range(N):
                for g in range(8):
                    v, i = np.unique(place[q, g], return_index=True)
                    X[q, g][:, v] = z[q, g][:, i]
        A = np.add.reduce((j == K).astype(np.int64), axis=(1, 2))
        steps.append(new); z = np.roll(new, 1, axis=0)
    return {"ym": M.reshape(N, 128, K * P).astype(np.float32).astype(BF), "yz": np.stack(steps, axis=3).reshape(N, 128, RO * P).astype(np.float32).astype(BF)}

@@ -1,0 +1,433 @@
+from concourse.mybir import dt, AluOpType, AxisListType, ActivationFunctionType
+
+A = AluOpType
+FN = ActivationFunctionType
+STEPS, NP, NK, NW, LIMIT = 6, 256, 8, 4096, 88
+MAGIC = 12582912.0
+B16, F32, I32, U16, F16 = "bfloat16", "float32", "int32", "uint16", "float16"
+MZV, MZS = (0, 1), (2, 3)
+SB = {0: 7, 2: 5}
+NOB = 3
+NSC = 5
+
+_SB = {
+    "tab": (NW + 16, B16), "mska": (2304, B16), "mskb": (2304, B16), "mz": (2048, B16), "yy": (2048, B16), "xh": (2048, B16),
+    "ab": (2048, B16), "ff": (2048, B16), "fr": (2048, B16), "mini": (8, B16), "wts": (2, B16), "ones": (512, B16),
+    "ident": (128, B16), "nident": (128, B16), "ident256": (128, B16), "idm512": (128, B16), "id600": (128, B16),
+    "idpow": (1024, B16), "triw": (128, B16), "sel": (144, B16), "bigu": (144, B16), "bigv": (144, B16),
+    "shf": (1920, B16), "shh": (1920, F16), "cmpt": (240, F32), "k4": (128, F32), "baseoff": (128, F32),
+    "qi": (8, I32), "qf": (8, F32), "dum": (8, F32), "m256": (8, F32), "sgn": (16, B16), "ctab": (8, F32), "thrt": (16, B16),
+    "hi0": (128, I32), "hi1": (128, I32), "hi2": (32, I32), "ha0": (64, I32), "ha1": (64, I32), "ha2": (16, I32),
+    "hb0": (64, I32), "hb1": (64, I32), "hb2": (16, I32), "hu0": (64, U16), "hu1": (64, U16), "bs0": (64, F32), "bs1": (64, F32),
+    "nk0": (64, F32), "nk1": (64, F32), "ky0": (64, F32), "ky1": (64, F32), "ka0": (32, F32), "ka1": (32, F32),
+    "kb0": (16, F32), "kb1": (16, F32), "key": (16, I32), "hs": (16, I32), "hsu": (16, U16), "nmu": (16, U16), "nmf": (16, B16),
+    "jr": (16, I32), "jru": (16, U16), "ob": (128, F32), "of": (128, F32), "offu": (128, U16),
+    "sz": (256, B16), "yh": (256, F32), "cc": (256, F32), "wh": (256, F32), "thr": (256, B16), "u1": (256, B16), "uz": (256, B16),
+    "asum": (1, F32), "ai": (8, I32), "lim": (8, F32), "pl": (16, I32), "hlb": (16, F16), "eq": (240, B16),
+    "lo": (16, F32), "so": (16, F32), "scu": (32, U16),
+}
+SCRATCH = {}
+for _n in _SB:
+    SCRATCH[_n] = ("sbuf", [128, _SB[_n][0]], _SB[_n][1])
+for _t in range(STEPS):
+    SCRATCH["zin%d" % _t] = ("sbuf", [128, NP], B16)
+    SCRATCH["nz%d" % _t] = ("sbuf", [128, NP], B16)
+for _b in range(8):
+    SCRATCH["ps%d" % _b] = ("psum", [128, 512], F32)
+
+SEMAPHORES = ["sv", "ss", "sp", "sg", "sent", "ldw", "ldm", "ldz", "ldx", "outs"] + ["arr%d" % t for t in range(1, STEPS)]
+
+
+def rank_program(g, core, T, topo):
+    rank = T.rank_of(core)
+    if rank is None:
+        return
+    nxt_core = T.cores[(rank + 1) % len(T.cores)]
+    prv_core = T.cores[(rank - 1) % len(T.cores)]
+    V, S, P = g.vector, g.scalar, g.tensor
+
+    semof = {"V": "sv", "S": "ss", "P": "sp", "G": "sg"}
+    waiter = {"V": V.wait_ge, "S": S.wait_ge, "P": P.wait_ge, "G": g.wait_ge, "Y": g.sync.wait_ge}
+    count = {"V": 0, "S": 0, "P": 0, "G": 0}
+    known = {"V": {}, "S": {}, "P": {}, "G": {}, "Y": {}}
+    snap, lastw, readers, bankuse = {}, {}, {}, {}
+
+    def hold(e, r, w, banks):
+        deps = {}
+
+        def dep(f, n):
+            if known[e].get(f, 0) < n and deps.get(f, 0) < n:
+                deps[f] = n
+        for tag in r:
+            if tag in lastw:
+                dep(*lastw[tag])
+        for tag in w:
+            if tag in lastw and (lastw[tag][0] != e or tag == "tab"):
+                dep(*lastw[tag])
+            for f, n in readers.get(tag, {}).items():
+                if f != e:
+                    dep(f, n)
+        for b in banks:
+            for f, n in bankuse.get(b, {}).items():
+                if f != e:
+                    dep(f, n)
+        for f in sorted(deps):
+            n = deps[f]
+            if any(f2 != f and snap.get((f2, n2), {}).get(f, 0) >= n for f2, n2 in deps.items()):
+                continue
+            waiter[e](T.sem[semof.get(f, f)], n)
+        for f, n in deps.items():
+            for f2, n2 in snap.get((f, n), {}).items():
+                if known[e].get(f2, 0) < n2:
+                    known[e][f2] = n2
+            known[e][f] = max(known[e].get(f, 0), n)
+
+    def note(f, n, r, w, banks):
+        for tag in w:
+            lastw[tag] = (f, n)
+            readers[tag] = {}
+        for tag in r:
+            readers.setdefault(tag, {})[f] = n
+        for b in banks:
+            bankuse.setdefault(b, {})[f] = n
+
+    def op(e, call, r, w, banks=(), **kw):
+        hold(e, r, w, banks)
+        count[e] += 1
+        n = count[e]
+        call(**kw).then_inc(T.sem[semof[e]], 1)
+        snap[(e, n)] = dict(known[e])
+        note(e, n, r, w, banks)
+
+    def dma(e, call, sem, val, r, w, **kw):
+        hold(e, r, w, ())
+        call(**kw).then_inc(T.sem[sem], 16)
+        note(sem, val, r, w, ())
+
+    def tt(out, in0, in1, o, r, w, banks=()):
+        op("V", V.tensor_tensor, r, w, banks, out=out, in0=in0, in1=in1, op=o)
+
+    def ts(out, in0, s1, o1, r, w, banks=(), s2=None, o2=None):
+        if o2 is None:
+            op("V", V.tensor_scalar, r, w, banks, out=out, in0=in0, scalar1=s1, scalar2=None, op0=o1)
+        else:
+            op("V", V.tensor_scalar, r, w, banks, out=out, in0=in0, scalar1=s1, scalar2=s2, op0=o1, op1=o2)
+
+    def cp(out, in_, r, w, banks=()):
+        op("V", V.tensor_copy, r, w, banks, out=out, in_=in_)
+
+    def act(out, in_, func, r, w, banks=(), **kw):
+        op("S", S.activation, r, w, banks, out=out, in_=in_, func=func, **kw)
+
+    def mm(b, c0, c1, lhsT, rhs, start, stop, r):
+        op("P", P.matmul, r, [("ps", b)], [b], out=ps[b][:, c0:c1], lhsT=lhsT, rhs=rhs, start=start, stop=stop)
+
+    def fill(ap, val, w):
+        op("V", V.memset, [], [w], ap=ap, constant=val)
+
+    def sel(n, pattern, cmp, val, base, mul):
+        op("G", g.affine_select, [n], [n], out=T[n][:], in_=T[n][:], pattern=pattern, compare_op=cmp, fill=val, base=base,
+           channel_multiplier=mul)
+
+    def iota(n, lo, hi, pattern, base, mul):
+        kw = {} if n == "qi" else {"allow_small_or_imprecise_dtypes": True}
+        op("G", g.iota, [], [n], out=T[n][:, lo:hi], pattern=pattern, base=base, channel_multiplier=mul, **kw)
+
+    tab, mz, yy, ab, ff, fr, xh = T["tab"], T["mz"], T["yy"], T["ab"], T["ff"], T["fr"], T["xh"]
+    msk = [T["mska"], T["mskb"]]
+    ps = [T["ps%d" % b] for b in range(8)]
+    ident, nident, idpow = T["ident"], T["nident"], T["idpow"]
+    zin = [T["zin%d" % t] for t in range(STEPS)]
+    nz = [T["nz%d" % t] for t in range(STEPS)]
+    mtags = [[("m", s, k) for k in range(9)] for s in range(2)]
+
+    def cols(b):
+        return slice(512 * b, 512 * b + 512)
+
+    def mb(t, b):
+        return mtags[t % 2][2 * b:2 * b + 2]
+
+    dma("S", g.scalar.dma_start, "ldx", 16, [], ["tab"], out=tab[:, 0:NW], in_=T["xr"][:])
+    dma("Y", g.sync.dma_start, "ldz", 16, [], ["z0"], out=zin[0][:], in_=T["z0"][:])
+    dma("Y", g.sync.dma_start, "ldm", 16, [], ["mini"], out=T["mini"][:], in_=T["m0"][:])
+    dma("Y", g.sync.dma_start, "ldw", 16, [], ["wts"], out=T["wts"][:], in_=T["wt"][:])
+
+    fill(T["sel"][:], 1.0, "sel")
+    fill(ident[:], 1.0, "ident")
+    fill(T["triw"][:], 1.0, "triw")
+    fill(T["ones"][:], 1.0, "ones")
+    fill(T["shf"][:], 0.0, "shf")
+    fill(msk[0][:, 2048:2304], 0.0, ("m", 0, 8))
+    fill(T["lim"][:], 1.5, "lim")
+    sel("sel", [[-16, 9], [-1000, 16]], A.is_ge, 0.0, 16, 1)
+    sel("sel", [[16, 9], [-1000, 16]], A.is_ge, 0.0, -1, -1)
+    sel("ident", [[1, 128]], A.is_equal, 0.0, 0, -1)
+    iota("k4", 0, 128, [[4096, 8], [0, 16]], 0, 0)
+    sel("triw", [[-16, 8], [0, 16]], A.is_ge, 0.0, 0, 1)
+    sel("triw", [[1, 128]], A.is_ge, 0.0, -1, -1)
+    sel("triw", [[1, 128]], A.not_equal, -1.0, 0, -1)
+    iota("qi", 0, 8, [[0, 8]], 0, 1)
+    iota("baseoff", 0, 112, [[256, 7], [16, 16]], 256, 0)
+    iota("baseoff", 112, 128, [[16, 16]], 0, 0)
+    iota("cmpt", 0, 240, [[1, 15], [0, 16]], 1, 0)
+    sel("shf", [[0, 15], [1, 128]], A.not_equal, -1.0, 0, -1)
+    sel("shf", [[-1, 15], [1, 128]], A.not_equal, 1.0, -1, -1)
+
+    for k in range(NK):
+        ts(mz[:, 256 * k:256 * k + 256], zin[0][:], T["mini"][:, k:k + 1], A.mult, ["z0", "mini"], [("mz", k // 2)])
+        if k == 3:
+            ts(T["bigu"][:], T["sel"][:], T["wts"][:, 0:1], A.mult, ["sel", "wts"], ["bigu"])
+            ts(T["bigv"][:], T["sel"][:], T["wts"][:, 1:2], A.mult, ["sel", "wts"], ["bigv"])
+
+    def constants_first():
+        ts(nident[:], ident[:], -1.0, A.mult, ["ident"], ["nident"])
+        ts(T["idm512"][:], ident[:], -512.0, A.mult, ["ident"], ["idm512"])
+        ts(T["id600"][:], ident[:], 600.0, A.mult, ["ident"], ["id600"])
+        for k in range(NK):
+            act(msk[0][:, 256 * k:256 * k + 256], msk[0][:, 2048:2304], FN.Identity, [("m", 0, 8), "mini"], [("m", 0, k)],
+                bias=T["mini"][:, k:k + 1])
+
+    def constants_mid():
+        fill(msk[1][:, 2048:2304], 0.0, ("m", 1, 8))
+        fill(T["sgn"][:, 0:1], -1.0, "sgn")
+        fill(T["sgn"][:, 1:16], 1.0, "sgn")
+        fill(T["ctab"][:, 0:1], 1.0, "ctab")
+        fill(T["ctab"][:, 1:8], 0.5 - 1.0 / 4096, "ctab")
+        for j in range(8):
+            fill(T["thrt"][:, j:j + 1], float(2 ** (8 - j)), "thrt")
+        fill(T["thrt"][:, 8:16], 1.0, "thrt")
+        fill(T["m256"][:], -256.0, "m256")
+        for k in range(NK):
+            ts(idpow[:, 128 * k:128 * k + 128], ident[:], float(2 ** (7 - k)), A.mult, ["ident"], ["idpow"])
+        ts(T["ident256"][:], ident[:], 256.0, A.mult, ["ident"], ["ident256"])
+
+    def constants_last():
+        ts(T["qi"][:], T["qi"][:], 15, A.bitwise_and, ["qi"], ["qi"])
+        cp(T["qf"][:], T["qi"][:], ["qi"], ["qf"])
+        ts(T["dum"][:], T["qf"][:], float(NW), A.add, ["qf"], ["dum"])
+        ts(T["baseoff"][:], T["baseoff"][:], T["qf"][:, 0:1], A.add, ["qf", "baseoff"], ["baseoff"])
+        ts(T["cmpt"][:], T["cmpt"][:], T["qf"][:, 0:1], A.is_gt, ["qf", "cmpt"], ["cmpt"], s2=99999.0, o2=A.mult)
+        cp(T["shh"][:], T["shf"][:], ["shf"], ["shh"])
+
+    def header(t):
+        for h in range(2):
+            mm(6, 256 * h, 256 * h + 256, ident[:], zin[t][:], True, True, ["ident", "z%d" % t])
+        if t > 0:
+            for b in MZV:
+                tt(mz[:, cols(b)], msk[t % 2][:, cols(b)], ps[6][:], A.mult, mb(t, b) + [("ps", 6)], [("mz", b)], [6])
+
+    def masked(t):
+        for b in MZS:
+            mm(b, 0, 512, T["ident256"][:], msk[t % 2][:, cols(b)], True, False, ["ident256"] + mb(t, b))
+        for b in MZS:
+            for h in range(2):
+                mm(b, 256 * h, 256 * h + 256, ident[:], zin[t][:], False, h == 1, ["ident", "z%d" % t])
+        for b in MZS:
+            act(mz[:, cols(b)], ps[b][:], FN.Relu, [("ps", b), "m256"], [("mz", b)], [b], bias=T["m256"][:, 0:1])
+
+    def tolist(bank, c0, n, src, lo, hi, wt, rtags):
+        for q in range(16):
+            mm(bank, c0, c0 + n, T[wt][:, 16 - q:144 - q], src[:, lo + q:hi:16], q == 0, q == 15, [wt] + rtags)
+
+    def hashing(x, bank, n):
+        a, b, c = "hi%d" % x, "ha%d" % x, "hb%d" % x
+        hi, ha, hb = T[a], T[b], T[c]
+        return [lambda: cp(hi[:], ps[bank][:, 0:2 * n], [("ps", bank)], [a], [bank]),
+                lambda: ts(hi[:], hi[:], 4095, A.bitwise_and, [a], [a]),
+                lambda: tt(ha[:], hi[:, 0:n], hi[:, n:2 * n], A.mult, [a], [b]),
+                lambda: ts(hb[:], hi[:, 0:n], 37.0, A.mult, [a], [c]),
+                lambda: ts(ha[:], ha[:], 5, A.arith_shift_right, [b], [b]),
+                lambda: tt(ha[:], ha[:], hb[:], A.add, [b, c], [b])]
+
+    def places(h):
+        ha, tag, hu = T["ha%d" % h], "ha%d" % h, "hu%d" % h
+        return hashing(h, 4 + h, 64) + [lambda: ts(ha[:], ha[:], 4095, A.bitwise_and, [tag], [tag]),
+                                        lambda: cp(T[hu][:], ha[:], [tag], [hu])]
+
+    def limits(t, b):
+        mm(SB[b], 0, 512, T["idm512"][:], msk[t % 2][:, cols(b)], True, False, ["idm512"] + mb(t, b))
+        mm(SB[b], 0, 512, T["id600"][:], T["ones"][:], False, True, ["id600", "ones"])
+
+    def merge(first, second):
+        n = max(len(first), len(second))
+        for i in range(n):
+            for chain in (first, second):
+                for f in chain[i * len(chain) // n:(i + 1) * len(chain) // n]:
+                    f()
+
+    def front(t, scatters):
+        for h in range(2):
+            rt = [("mz", 2 * h), ("mz", 2 * h + 1)]
+            tolist(4 + h, 0, 64, mz, 1024 * h, 1024 * h + 1024, "bigu", rt)
+            tolist(4 + h, 64, 64, mz, 1024 * h, 1024 * h + 1024, "bigv", rt)
+        if t == 0:
+            header(0)
+            constants_first()
+        for b in range(4):
+            if b not in SB:
+                mm(b, 0, 512, nident[:], mz[:, cols(b)], True, False, ["nident", ("mz", b)])
+        limits(t, 0)
+        merge([], scatters[:NSC])
+        merge(places(0) + places(1), scatters[NSC:])
+        if t == 0:
+            constants_mid()
+        limits(t, 2)
+
+    def gathermask(t, b):
+        h, o = b // 2, 32 * (b % 2)
+        hu = "hu%d" % h
+        win = tab[:, 0:NW].indirect(T[hu][:, o:o + 32])
+        if b in SB:
+            act(xh[:, cols(b)], win, FN.Copy, ["tab", hu], [("xh", b)])
+        else:
+            tt(yy[:, cols(b)], win, msk[t % 2][:, cols(b)], A.mult, ["tab", hu] + mb(t, b), [("yy", b)])
+
+    def difference(t, b):
+        if b in SB:
+            mm(b, 0, 512, ident[:], xh[:, cols(b)], True, False, ["ident", ("xh", b)])
+            for h in range(2):
+                mm(b, 256 * h, 256 * h + 256, nident[:], zin[t][:], False, h == 1, ["nident", "z%d" % t])
+        else:
+            mm(b, 0, 512, ident[:], yy[:, cols(b)], False, True, ["ident", ("yy", b)])
+
+    def absol(b):
+        act(ab[:, cols(b)], ps[b][:], FN.Abs, [("ps", b)], [("ab", b)], [b])
+
+    def failing(b):
+        if b in SB:
+            tt(ff[:, cols(b)], ab[:, cols(b)], ps[SB[b]][:], A.is_gt, [("ab", b), ("ps", SB[b])], [("ff", b)], [SB[b]])
+        else:
+            ts(ff[:, cols(b)], ab[:, cols(b)], float(LIMIT), A.is_gt, [("ab", b)], [("ff", b)])
+
+    def prefix(b):
+        mm(b, 0, 512, T["triw"][:], ff[:, cols(b)], True, True, ["triw", ("ff", b)])
+
+    def firsts(b):
+        act(fr[:, cols(b)], ps[b][:], FN.Relu, [("ps", b)], [("fr", b)], [b], scale=-1.0)
+
+    def counts(h):
+        tolist(4 + h, 0, 64, ff, 1024 * h, 1024 * h + 1024, "sel", [("ff", 2 * h), ("ff", 2 * h + 1)])
+
+    def bases(h):
+        x = str(h)
+        tt(T["bs" + x][:], T["ha" + x][:], T["k4"][:, 64 * h:64 * h + 64], A.add, ["ha" + x, "k4"], ["bs" + x])
+
+    def keys(h):
+        x = str(h)
+        ts(T["nk" + x][:], ps[4 + h][:, 0:64], T["lim"][:, 0:1], A.is_gt, [("ps", 4 + h), "lim"], ["nk" + x], [4 + h],
+           s2=32768.0, o2=A.mult)
+        tt(T["ky" + x][:], T["nk" + x][:], T["bs" + x][:], A.add, ["nk" + x, "bs" + x], ["ky" + x])
+        tt(T["ka" + x][:], T["ky" + x][:, 0:32], T["ky" + x][:, 32:64], A.min, ["ky" + x], ["ka" + x])
+        tt(T["kb" + x][:], T["ka" + x][:, 0:16], T["ka" + x][:, 16:32], A.min, ["ka" + x], ["kb" + x])
+
+    def moves(ks):
+        for k in ks:
+            if k == NK:
+                ts(T["ob"][:, 112:128], T["jr"][:], 8.0, A.min, ["jr"], ["ob"], s2=256.0, o2=A.mult)
+            else:
+                ts(T["ob"][:, 16 * k - 16:16 * k], T["jr"][:], float(k), A.is_ge, ["jr"], ["ob"], s2=-256.0, o2=A.mult)
+
+    def scatter(t, c):
+        return lambda: cp(tab[:].indirect(T["scu"][:, 2 * c:2 * c + 1]), zin[t][:, 16 * c:16 * c + 16], ["scu", "z%d" % t], ["tab"])
+
+    front(0, [])
+    for t in range(STEPS):
+        zt, s2 = "z%d" % t, (t + 1) % 2
+        cur, nxt, ctags, ntags = msk[t % 2], msk[s2], mtags[t % 2], mtags[s2]
+        last = t == STEPS - 1
+        for b in range(4):
+            gathermask(t, b)
+        if t == 0:
+            constants_last()
+        for b in range(4):
+            difference(t, b)
+            absol(b)
+        failing(0)
+        prefix(0)
+        failing(1)
+        counts(0)
+        bases(0)
+        bases(1)
+        prefix(1)
+        failing(2)
+        prefix(2)
+        failing(3)
+        counts(1)
+        prefix(3)
+        firsts(0)
+        firsts(1)
+        firsts(2)
+        keys(0)
+        keys(1)
+        tt(T["key"][:], T["kb0"][:], T["kb1"][:], A.min, ["kb0", "kb1"], ["key"])
+        ts(T["nmu"][:], T["key"][:], 32768.0, A.is_ge, ["key"], ["nmu"])
+        ts(T["hs"][:], T["key"][:], 4095, A.bitwise_and, ["key"], ["hs"])
+        tt(T["sz"][:], T["sgn"][:].indirect(T["nmu"][:]), zin[t][:], A.mult, ["sgn", "nmu", zt], ["sz"])
+        cp(T["hsu"][:], T["hs"][:], ["hs"], ["hsu"])
+        act(T["cc"][:], T["ctab"][:].indirect(T["nmu"][:]), FN.Copy, ["ctab", "nmu"], ["cc"])
+        tt(T["yh"][:], tab[:, 0:NW].indirect(T["hsu"][:]), T["sz"][:], A.add, ["tab", "hsu", "sz"], ["yh"])
+        firsts(3)
+        act(ps[7][:, 0:256], T["yh"][:], FN.Abs, ["yh"], [("ps", 7)], [7])
+        ts(T["jr"][:], T["key"][:], 12, A.arith_shift_right, ["key"], ["jr"])
+        if not last:
+            ts(T["nmf"][:], T["key"][:], 32768.0, A.is_ge, ["key"], ["nmf"])
+        cp(T["jru"][:], T["jr"][:], ["jr"], ["jru"])
+        act(T["thr"][:], T["thrt"][:].indirect(T["jru"][:]), FN.Copy, ["thrt", "jru"], ["thr"])
+        moves(range(1, 1 + NOB))
+        tt(T["wh"][:], T["cc"][:], ps[7][:, 0:256], A.mult, ["cc", ("ps", 7)], ["wh"], [7])
+        ts(nz[t][:], T["wh"][:], MAGIC, A.add, ["wh"], [("nz", t)], s2=-MAGIC, o2=A.add)
+        if not last:
+            rid, pid = topo.addr(nxt_core, core)
+            hold("G", [("nz", t)], [], ())
+            g.remote_dma(out_ap=zin[t + 1][:], in_ap=nz[t][:], remote_sem=T.sem["arr%d" % (t + 1)], local_sem=T.sem["sent"],
+                         pid=pid, routing_id=rid, dma_engine_mask=topo.mask(core, nxt_core))
+            lastw["z%d" % (t + 1)] = ("arr%d" % (t + 1), len(topo.engines(prv_core, core)))
+        dma("Y", g.sync.dma_start, "outs", 16 * (t + 1), [("nz", t)], [], out=T["yz"][:, NP * t:NP * t + NP], in_=nz[t][:])
+        moves(range(1 + NOB, 9))
+        tt(T["of"][:], T["ob"][:], T["baseoff"][:], A.add, ["ob", "baseoff"], ["of"])
+        if not last:
+            mm(4, 256, 272, T["ones"][:, 0:128], T["nmf"][:], True, True, ["ones", "nmf"])
+        for k in range(NK):
+            mm(4, 0, 256, idpow[:, 128 * k:128 * k + 128], fr[:, 256 * k:256 * k + 256], k == 0, k == NK - 1,
+               ["idpow", ("fr", k // 2)])
+        tt(T["u1"][:], T["thr"][:], ps[4][:, 0:256], A.is_le, ["thr", ("ps", 4)], ["u1"], [4])
+        cp(T["offu"][:], T["of"][:], ["of"], ["offu"])
+        low = cur[:].indirect(T["offu"][:, 0:48])
+        if not last:
+            act(nxt[:, 256:1024], low, FN.Copy, ctags + ["offu"], ntags[1:4])
+        act(nxt[:, 1024:2048], cur[:].indirect(T["offu"][:, 48:112]), FN.Copy, ctags + ["offu"], ntags[4:8])
+        tt(nxt[:, 0:256], cur[:].indirect(T["offu"][:, 112:128]), T["u1"][:], A.max, ctags + ["offu", "u1"], [ntags[0]])
+        if last:
+            cp(nxt[:, 256:1024], low, ctags + ["offu"], ntags[1:4])
+            break
+        tt(T["uz"][:], nxt[:, 0:256], ps[6][:, 0:256], A.mult, [ntags[0], ("ps", 6)], ["uz"], [6])
+        tolist(5, 0, 16, T["uz"], 0, 256, "bigu", ["uz"])
+        tolist(5, 16, 16, T["uz"], 0, 256, "bigv", ["uz"])
+        op("V", V.tensor_reduce, [("ps", 4)], ["asum"], [4], out=T["asum"][:], in_=ps[4][:, 256:272], axis=AxisListType.X, op=A.add)
+        cp(T["ai"][:, 0:1], T["asum"][:], ["asum"], ["ai"])
+        ts(T["ai"][:, 0:1], T["ai"][:, 0:1], 1, A.bitwise_and, ["ai"], ["ai"])
+        ts(T["lim"][:, 0:1], T["ai"][:, 0:1], 1.5, A.add, ["ai"], ["lim"])
+        for f in hashing(2, 5, 16):
+            f()
+        ts(T["pl"][:], T["ha2"][:], 4095, A.bitwise_and, ["ha2"], ["pl"])
+        ts(T["hlb"][:], T["pl"][:], -2048.0, A.add, ["pl"], ["hlb"])
+        header(t + 1)
+        for d in range(15):
+            mm(7, 16 * d, 16 * d + 16, T["shh"][:, 128 * d:128 * d + 128], T["hlb"][:], True, True, ["shh", "hlb"])
+        masked(t + 1)
+        tt(T["eq"][:], T["cmpt"][:], ps[7][:, 0:240], A.is_equal, ["cmpt", ("ps", 7)], ["eq"], [7])
+        for d in range(15):
+            mm(5, 32, 48, ident[:], T["eq"][:, 16 * d:16 * d + 16], d == 0, d == 14, ["ident", "eq"])
+        ts(T["lo"][:], ps[5][:, 32:48], 0.5, A.is_gt, [("ps", 5), "dum"], ["lo"], [5], s2=T["dum"][:, 0:1], o2=A.mult)
+        tt(T["so"][:], T["lo"][:], T["pl"][:], A.max, ["lo", "pl"], ["so"])
+        cp(T["scu"][:, 0:32:2], T["so"][:], ["so"], ["scu"])
+        front(t + 1, [scatter(t, c) for c in range(15, -1, -1)])
+    s2 = STEPS % 2
+    n = 16 * STEPS
+    for lo, hi, tags in ((0, 256, mtags[s2][0:1]), (256, 1024, mtags[s2][1:4]), (1024, 2048, mtags[s2][4:8])):
+        n += 16
+        dma("Y", g.sync.dma_start, "outs", n, tags, [], out=T["ym"][:, lo:hi], in_=msk[s2][:, lo:hi])
+    g.sync.wait_ge(T.sem["outs"], n)
+    for e in ("V", "S", "P", "G"):
+        g.sync.wait_ge(T.sem[semof[e]], count[e])
+    g.wait_ge(T.sem["sent"], (STEPS - 1) * len(topo.engines(core, nxt_core)))

@@ -1,41 +1,56 @@
+import numpy as np
 from concourse.mybir import dt, AluOpType, AxisListType, ActivationFunctionType
 
 A = AluOpType
 FN = ActivationFunctionType
-STEPS, NP, NK, NW, LIMIT = 6, 256, 8, 4096, 88
+STEPS, NP, NK, NW = 6, 256, 8, 4096
 MAGIC = 12582912.0
+SLOPE = 185.0 / 32768
+OFF = 4096.0
+WIPE = 2.0 ** 22
+BIG = 2.0 ** 25
+HALF = 2.0 ** 23
 B16, F32, I32, U16, F16 = "bfloat16", "float32", "int32", "uint16", "float16"
-MZV, MZS = (0, 1), (2, 3)
-SB = {0: 7, 2: 5}
-NOB = 3
-NSC = 5
+SG = (0, 2)
+FS = (2,)
+BLK = 3
+BLOCKS = [list(range(c, min(c + BLK, 16))) for c in range(0, 16, BLK)]
+PAIRS = [(c, o) for blk in BLOCKS for c in blk for o in range(c, blk[0] - 1, -1)]
+NPAIR = len(PAIRS)
+WD = 16 * NPAIR
+PERIOD = BLK * (BLK + 1) // 2
 
 _SB = {
-    "tab": (NW + 16, B16), "mska": (2304, B16), "mskb": (2304, B16), "mz": (2048, B16), "yy": (2048, B16), "xh": (2048, B16),
-    "ab": (2048, B16), "ff": (2048, B16), "fr": (2048, B16), "mini": (8, B16), "wts": (2, B16), "ones": (512, B16),
-    "ident": (128, B16), "nident": (128, B16), "ident256": (128, B16), "idm512": (128, B16), "id600": (128, B16),
-    "idpow": (1024, B16), "triw": (128, B16), "sel": (144, B16), "bigu": (144, B16), "bigv": (144, B16),
-    "shf": (1920, B16), "shh": (1920, F16), "cmpt": (240, F32), "k4": (128, F32), "baseoff": (128, F32),
-    "qi": (8, I32), "qf": (8, F32), "dum": (8, F32), "m256": (8, F32), "sgn": (16, B16), "ctab": (8, F32), "thrt": (16, B16),
-    "hi0": (128, I32), "hi1": (128, I32), "hi2": (32, I32), "ha0": (64, I32), "ha1": (64, I32), "ha2": (16, I32),
-    "hb0": (64, I32), "hb1": (64, I32), "hb2": (16, I32), "hu0": (64, U16), "hu1": (64, U16), "bs0": (64, F32), "bs1": (64, F32),
-    "nk0": (64, F32), "nk1": (64, F32), "ky0": (64, F32), "ky1": (64, F32), "ka0": (32, F32), "ka1": (32, F32),
-    "kb0": (16, F32), "kb1": (16, F32), "key": (16, I32), "hs": (16, I32), "hsu": (16, U16), "nmu": (16, U16), "nmf": (16, B16),
-    "jr": (16, I32), "jru": (16, U16), "ob": (128, F32), "of": (128, F32), "offu": (128, U16),
-    "sz": (256, B16), "yh": (256, F32), "cc": (256, F32), "wh": (256, F32), "thr": (256, B16), "u1": (256, B16), "uz": (256, B16),
-    "asum": (1, F32), "ai": (8, I32), "lim": (8, F32), "pl": (16, I32), "hlb": (16, F16), "eq": (240, B16),
-    "lo": (16, F32), "so": (16, F32), "scu": (32, U16),
+    "tab": (NW + NP, B16), "na": (2048, B16), "nb": (2048, B16), "th": (2064, B16), "mz": (2048, B16), "xy": (2048, B16),
+    "ff": (2048, B16), "fr": (2048, B16), "mini": (8, B16), "wts": (2, B16), "ones": (512, B16), "n0": (8, F32), "th0": (8, F32),
+    "ident": (128, B16), "slope": (128, B16), "nslope": (128, B16), "wipe": (128, B16), "nwipe": (128, B16), "half": (128, B16),
+    "nhalf": (128, B16), "quart": (128, B16), "magic": (128, B16), "nbig": (128, B16), "idpow": (1024, B16), "triw": (128, B16),
+    "sel": (144, B16), "bigu": (144, B16), "bigv": (144, B16), "bigc": (144, B16), "blk": (128, B16), "neg": (128, B16),
+    "rot": (2048, F16), "nid": (128, F16), "rti": (128, I32), "rtf": (128, F32), "inval": (WD, B16), "clamp": (16 * PERIOD * len(BLOCKS), F32),
+    "qi": (8, I32), "qf": (8, F32), "cb": (8, F32), "jc": (144, F32), "kc": (128, F32), "kge": (112, F32), "mvb": (112, F32),
+    "none": (32, F32), "tmp": (16, F32), "row": (128, F32), "lrep": (8, U16), "lpair": (4, U16), "lslot": (2, U16), "lend": (2, U16),
+    "hi0": (128, I32), "hi1": (128, I32), "hi2": (32, I32), "hp": (128, I32), "hq": (128, I32), "hh": (128, I32), "hu": (128, U16),
+    "gp": (16, I32), "gq": (16, I32), "pl": (16, I32), "base": (128, F32), "ky": (128, F32), "ka": (32, F32), "kb": (32, F32),
+    "kc2": (32, F32), "kd": (32, F32), "key": (16, I32), "hs": (16, I32), "hsu": (16, U16), "ju": (16, U16), "nm": (16, B16),
+    "ge": (112, F32), "mv": (112, F32), "mvu": (112, U16), "ssb": (256, B16), "ub": (256, B16), "uz": (256, B16),
+    "hx": (64, F16), "eq": (WD, B16), "st": (WD, F32), "scu": (32, U16), "par": (16, F32), "px": (8, F32), "lim": (64, B16),
+    "two": (64, B16), "mo": (2048, B16), "cnt": (16, F32), "dg": (32, F32), "lf": (8, F32),
+    "ro": (36, F32), "rc": (36, F32), "rs": (18, F32), "re": (32, F32),
 }
 SCRATCH = {}
 for _n in _SB:
     SCRATCH[_n] = ("sbuf", [128, _SB[_n][0]], _SB[_n][1])
 for _t in range(STEPS):
-    SCRATCH["zin%d" % _t] = ("sbuf", [128, NP], B16)
+    SCRATCH["zb%d" % _t] = ("sbuf", [128, NP], B16)
+    SCRATCH["dz%d" % _t] = ("sbuf", [128, NP], B16)
     SCRATCH["nz%d" % _t] = ("sbuf", [128, NP], B16)
+    if _t:
+        SCRATCH["zs%d" % _t] = ("sbuf", [128, NP], B16)
 for _b in range(8):
     SCRATCH["ps%d" % _b] = ("psum", [128, 512], F32)
 
 SEMAPHORES = ["sv", "ss", "sp", "sg", "sent", "ldw", "ldm", "ldz", "ldx", "outs"] + ["arr%d" % t for t in range(1, STEPS)]
+QUEUES = ("V", "S", "P", "G")
 
 
 def rank_program(g, core, T, topo):
@@ -46,388 +61,416 @@ def rank_program(g, core, T, topo):
     prv_core = T.cores[(rank - 1) % len(T.cores)]
     V, S, P = g.vector, g.scalar, g.tensor
 
+    def R(name, lo=0, hi=None, step=1):
+        return (name, lo, SCRATCH[name][1][1] if hi is None else hi, step)
+
+    def G(win, off):
+        return win + (off,)
+
+    def ap(r):
+        a = T[r[0]][:, r[1]:r[2]:r[3]] if r[3] != 1 else T[r[0]][:, r[1]:r[2]]
+        return a.indirect(ap(r[4])) if len(r) > 4 else a
+
     semof = {"V": "sv", "S": "ss", "P": "sp", "G": "sg"}
     waiter = {"V": V.wait_ge, "S": S.wait_ge, "P": P.wait_ge, "G": g.wait_ge, "Y": g.sync.wait_ge}
     count = {"V": 0, "S": 0, "P": 0, "G": 0}
     known = {"V": {}, "S": {}, "P": {}, "G": {}, "Y": {}}
-    snap, lastw, readers, bankuse = {}, {}, {}, {}
+    snap, wrote, read, bank = {}, {}, {}, {}
 
-    def hold(e, r, w, banks):
+    def marks(book, r):
+        return [(f, int(a[r[1]:r[2]].max())) for f, a in book.get(r[0], {}).items()]
+
+    def hold(e, rd, wr):
         deps = {}
-
-        def dep(f, n):
-            if known[e].get(f, 0) < n and deps.get(f, 0) < n:
+        found = []
+        for r in rd:
+            found += marks(wrote, r)
+        for r in wr:
+            found += marks(wrote, r) + marks(read, r)
+        for r in rd + wr:
+            found += [x for x in bank.get(r[0], {}).items() if x[0] != e]
+        for f, n in found:
+            if not (e == "P" and f == "P") and known[e].get(f, 0) < n and deps.get(f, 0) < n:
                 deps[f] = n
-        for tag in r:
-            if tag in lastw:
-                dep(*lastw[tag])
-        for tag in w:
-            if tag in lastw and (lastw[tag][0] != e or tag == "tab"):
-                dep(*lastw[tag])
-            for f, n in readers.get(tag, {}).items():
-                if f != e:
-                    dep(f, n)
-        for b in banks:
-            for f, n in bankuse.get(b, {}).items():
-                if f != e:
-                    dep(f, n)
         for f in sorted(deps):
-            n = deps[f]
-            if any(f2 != f and snap.get((f2, n2), {}).get(f, 0) >= n for f2, n2 in deps.items()):
-                continue
-            waiter[e](T.sem[semof.get(f, f)], n)
+            if not any(f2 != f and snap.get((f2, n2), {}).get(f, 0) >= deps[f] for f2, n2 in deps.items()):
+                waiter[e](T.sem[semof.get(f, f)], deps[f])
         for f, n in deps.items():
             for f2, n2 in snap.get((f, n), {}).items():
-                if known[e].get(f2, 0) < n2:
-                    known[e][f2] = n2
+                known[e][f2] = max(known[e].get(f2, 0), n2)
             known[e][f] = max(known[e].get(f, 0), n)
 
-    def note(f, n, r, w, banks):
-        for tag in w:
-            lastw[tag] = (f, n)
-            readers[tag] = {}
-        for tag in r:
-            readers.setdefault(tag, {})[f] = n
-        for b in banks:
-            bankuse.setdefault(b, {})[f] = n
+    def note(f, n, rd, wr):
+        for book, rs in ((read, rd), (wrote, wr)):
+            for r in rs:
+                if SCRATCH[r[0]][0] == "psum":
+                    bank.setdefault(r[0], {})[f] = n
+                marks_of = book.setdefault(r[0], {})
+                if f not in marks_of:
+                    marks_of[f] = np.zeros(SCRATCH[r[0]][1][1], np.int64)
+                marks_of[f][r[1]:r[2]] = n
 
-    def op(e, call, r, w, banks=(), **kw):
-        hold(e, r, w, banks)
+    def op(e, call, outs, **kw):
+        wr = [kw[k] for k in outs]
+        rd = [v for k, v in kw.items() if isinstance(v, tuple) and k not in outs]
+        rd += [r[4] for r in rd + wr if len(r) > 4]
+        hold(e, rd, wr)
         count[e] += 1
-        n = count[e]
-        call(**kw).then_inc(T.sem[semof[e]], 1)
-        snap[(e, n)] = dict(known[e])
-        note(e, n, r, w, banks)
+        call(**{k: ap(v) if isinstance(v, tuple) else v for k, v in kw.items()}).then_inc(T.sem[semof[e]], 1)
+        snap[(e, count[e])] = dict(known[e])
+        note(e, count[e], rd, wr)
 
-    def dma(e, call, sem, val, r, w, **kw):
-        hold(e, r, w, ())
-        call(**kw).then_inc(T.sem[sem], 16)
-        note(sem, val, r, w, ())
+    def load(q, sem, r, src):
+        q.dma_start(out=ap(r), in_=src).then_inc(T.sem[sem], 16)
+        note(sem, 16, [], [r])
 
-    def tt(out, in0, in1, o, r, w, banks=()):
-        op("V", V.tensor_tensor, r, w, banks, out=out, in0=in0, in1=in1, op=o)
+    stored = [0]
 
-    def ts(out, in0, s1, o1, r, w, banks=(), s2=None, o2=None):
-        if o2 is None:
-            op("V", V.tensor_scalar, r, w, banks, out=out, in0=in0, scalar1=s1, scalar2=None, op0=o1)
-        else:
-            op("V", V.tensor_scalar, r, w, banks, out=out, in0=in0, scalar1=s1, scalar2=s2, op0=o1, op1=o2)
+    def store(dst, r):
+        hold("Y", [r], [])
+        g.sync.dma_start(out=dst, in_=ap(r)).then_inc(T.sem["outs"], 16)
+        stored[0] += 16
 
-    def cp(out, in_, r, w, banks=()):
-        op("V", V.tensor_copy, r, w, banks, out=out, in_=in_)
+    def tt(out, in0, in1, o):
+        op("V", V.tensor_tensor, ["out"], out=out, in0=in0, in1=in1, op=o)
 
-    def act(out, in_, func, r, w, banks=(), **kw):
-        op("S", S.activation, r, w, banks, out=out, in_=in_, func=func, **kw)
+    def ts(out, in0, s1, o1, s2=None, o2=None):
+        more = {} if o2 is None else {"op1": o2}
+        op("V", V.tensor_scalar, ["out"], out=out, in0=in0, scalar1=s1, scalar2=s2, op0=o1, **more)
 
-    def mm(b, c0, c1, lhsT, rhs, start, stop, r):
-        op("P", P.matmul, r, [("ps", b)], [b], out=ps[b][:, c0:c1], lhsT=lhsT, rhs=rhs, start=start, stop=stop)
+    def cp(out, in_):
+        op("V", V.tensor_copy, ["out"], out=out, in_=in_)
 
-    def fill(ap, val, w):
-        op("V", V.memset, [], [w], ap=ap, constant=val)
+    def act(out, in_, func, **kw):
+        op("S", S.activation, ["out"] + [k for k in kw if k == "accum_out"], out=out, in_=in_, func=func, **kw)
 
-    def sel(n, pattern, cmp, val, base, mul):
-        op("G", g.affine_select, [n], [n], out=T[n][:], in_=T[n][:], pattern=pattern, compare_op=cmp, fill=val, base=base,
+    def mm(out, lhsT, rhs, start, stop):
+        op("P", P.matmul, ["out"], out=out, lhsT=lhsT, rhs=rhs, start=start, stop=stop)
+
+    def fill(r, val):
+        op("V", V.memset, ["ap"], ap=r, constant=val)
+
+    def select(n, pattern, cmp, val, base, mul):
+        op("G", g.affine_select, ["out"], out=R(n), in_=R(n), pattern=pattern, compare_op=cmp, fill=val, base=base,
            channel_multiplier=mul)
 
-    def iota(n, lo, hi, pattern, base, mul):
-        kw = {} if n == "qi" else {"allow_small_or_imprecise_dtypes": True}
-        op("G", g.iota, [], [n], out=T[n][:, lo:hi], pattern=pattern, base=base, channel_multiplier=mul, **kw)
+    def iota(r, pattern, base, mul):
+        kw = {} if SCRATCH[r[0]][2] == I32 else {"allow_small_or_imprecise_dtypes": True}
+        op("G", g.iota, ["out"], out=r, pattern=pattern, base=base, channel_multiplier=mul, **kw)
 
-    tab, mz, yy, ab, ff, fr, xh = T["tab"], T["mz"], T["yy"], T["ab"], T["ff"], T["fr"], T["xh"]
-    msk = [T["mska"], T["mskb"]]
-    ps = [T["ps%d" % b] for b in range(8)]
-    ident, nident, idpow = T["ident"], T["nident"], T["idpow"]
-    zin = [T["zin%d" % t] for t in range(STEPS)]
-    nz = [T["nz%d" % t] for t in range(STEPS)]
-    mtags = [[("m", s, k) for k in range(9)] for s in range(2)]
+    def ps(b, lo=0, hi=512, step=1):
+        return ("ps%d" % b, lo, hi, step)
 
-    def cols(b):
-        return slice(512 * b, 512 * b + 512)
+    def bk(name, b):
+        return R(name, 512 * b, 512 * b + 512)
 
-    def mb(t, b):
-        return mtags[t % 2][2 * b:2 * b + 2]
+    def mk(name, k):
+        return R(name, 256 * k, 256 * k + 256)
 
-    dma("S", g.scalar.dma_start, "ldx", 16, [], ["tab"], out=tab[:, 0:NW], in_=T["xr"][:])
-    dma("Y", g.sync.dma_start, "ldz", 16, [], ["z0"], out=zin[0][:], in_=T["z0"][:])
-    dma("Y", g.sync.dma_start, "ldm", 16, [], ["mini"], out=T["mini"][:], in_=T["m0"][:])
-    dma("Y", g.sync.dma_start, "ldw", 16, [], ["wts"], out=T["wts"][:], in_=T["wt"][:])
+    def col(name, j):
+        return R(name, j, j + 1)
 
-    fill(T["sel"][:], 1.0, "sel")
-    fill(ident[:], 1.0, "ident")
-    fill(T["triw"][:], 1.0, "triw")
-    fill(T["ones"][:], 1.0, "ones")
-    fill(T["shf"][:], 0.0, "shf")
-    fill(msk[0][:, 2048:2304], 0.0, ("m", 0, 8))
-    fill(T["lim"][:], 1.5, "lim")
-    sel("sel", [[-16, 9], [-1000, 16]], A.is_ge, 0.0, 16, 1)
-    sel("sel", [[16, 9], [-1000, 16]], A.is_ge, 0.0, -1, -1)
-    sel("ident", [[1, 128]], A.is_equal, 0.0, 0, -1)
-    iota("k4", 0, 128, [[4096, 8], [0, 16]], 0, 0)
-    sel("triw", [[-16, 8], [0, 16]], A.is_ge, 0.0, 0, 1)
-    sel("triw", [[1, 128]], A.is_ge, 0.0, -1, -1)
-    sel("triw", [[1, 128]], A.not_equal, -1.0, 0, -1)
-    iota("qi", 0, 8, [[0, 8]], 0, 1)
-    iota("baseoff", 0, 112, [[256, 7], [16, 16]], 256, 0)
-    iota("baseoff", 112, 128, [[16, 16]], 0, 0)
-    iota("cmpt", 0, 240, [[1, 15], [0, 16]], 1, 0)
-    sel("shf", [[0, 15], [1, 128]], A.not_equal, -1.0, 0, -1)
-    sel("shf", [[-1, 15], [1, 128]], A.not_equal, 1.0, -1, -1)
+    nbuf = ["na", "nb"]
+    NMAGIC, POFF, ONE, P175, M64, PMAGIC = (col("cb", j) for j in range(6))
 
-    for k in range(NK):
-        ts(mz[:, 256 * k:256 * k + 256], zin[0][:], T["mini"][:, k:k + 1], A.mult, ["z0", "mini"], [("mz", k // 2)])
-        if k == 3:
-            ts(T["bigu"][:], T["sel"][:], T["wts"][:, 0:1], A.mult, ["sel", "wts"], ["bigu"])
-            ts(T["bigv"][:], T["sel"][:], T["wts"][:, 1:2], A.mult, ["sel", "wts"], ["bigv"])
+    load(g.sync, "ldz", R("zb0"), T["z0"][:])
+    load(g.scalar, "ldm", R("mini"), T["m0"][:])
+    load(g.sync, "ldw", R("wts"), T["wt"][:])
+    load(g.scalar, "ldx", R("tab", 0, NW), T["xr"][:])
 
-    def constants_first():
-        ts(nident[:], ident[:], -1.0, A.mult, ["ident"], ["nident"])
-        ts(T["idm512"][:], ident[:], -512.0, A.mult, ["ident"], ["idm512"])
-        ts(T["id600"][:], ident[:], 600.0, A.mult, ["ident"], ["id600"])
+    def constants_start():
+        for n in ("sel", "ident", "triw", "ones"):
+            fill(R(n), 1.0)
+        for n in ("blk", "inval", "re"):
+            fill(R(n), 0.0)
+        for j, v in enumerate((-MAGIC, OFF, 1.0, 1.75, -1.0 / 64, MAGIC)):
+            fill(col("cb", j), v)
+        fill(R("lim"), 1.25)
+        fill(R("th", 2048, 2064), 1.0)
+        fill(R("two"), 2.0)
+        select("ident", [[1, 128]], A.is_equal, 0.0, 0, -1)
+        select("sel", [[-16, 9], [-1000, 16]], A.is_ge, 0.0, 16, 1)
+        iota(R("qi"), [[0, 8]], 0, 1)
+        select("sel", [[16, 9], [-1000, 16]], A.is_ge, 0.0, -1, -1)
+        iota(R("jc"), [[256, 9], [16, 16]], 0, 0)
+        select("blk", [[-16, 8], [0, 16]], A.is_ge, 100.0, 0, 1)
+        iota(R("cnt"), [[1, 16]], 0, 0)
+        select("blk", [[16, 8], [0, 16]], A.is_ge, 100.0, 15, -1)
+        iota(R("rti"), [[1, 128]], 128, -1)
+        select("triw", [[-16, 8], [0, 16]], A.is_ge, 0.0, 0, 1)
+        iota(R("kge"), [[256, 7], [0, 16]], 256, 0)
+        select("triw", [[1, 128]], A.is_ge, 0.0, -1, -1)
+        iota(R("clamp"), [[0, len(BLOCKS)], [-16, PERIOD], [0, 16]], NW + 16 * (PERIOD - 1), 1)
+        select("triw", [[1, 128]], A.not_equal, -1.0, 0, -1)
+        for n, v in (("wipe", WIPE), ("nslope", -SLOPE), ("slope", SLOPE), ("nwipe", -WIPE), ("nbig", -BIG), ("half", 0.5),
+                     ("quart", 0.25), ("nhalf", -0.5), ("magic", MAGIC), ("neg", -1.0)):
+            act(R(n), R("ident"), FN.Copy, scale=v)
+        ts(R("qi"), R("qi"), 15, A.bitwise_and)
+        ts(R("nid"), R("ident"), -1.0, A.mult)
+        cp(R("qf"), R("qi"))
+        cp(R("lrep"), R("qi"))
+
+    def constants_key():
+        ts(R("bigc"), R("sel"), BIG, A.mult)
         for k in range(NK):
-            act(msk[0][:, 256 * k:256 * k + 256], msk[0][:, 2048:2304], FN.Identity, [("m", 0, 8), "mini"], [("m", 0, k)],
-                bias=T["mini"][:, k:k + 1])
-
-    def constants_mid():
-        fill(msk[1][:, 2048:2304], 0.0, ("m", 1, 8))
-        fill(T["sgn"][:, 0:1], -1.0, "sgn")
-        fill(T["sgn"][:, 1:16], 1.0, "sgn")
-        fill(T["ctab"][:, 0:1], 1.0, "ctab")
-        fill(T["ctab"][:, 1:8], 0.5 - 1.0 / 4096, "ctab")
-        for j in range(8):
-            fill(T["thrt"][:, j:j + 1], float(2 ** (8 - j)), "thrt")
-        fill(T["thrt"][:, 8:16], 1.0, "thrt")
-        fill(T["m256"][:], -256.0, "m256")
-        for k in range(NK):
-            ts(idpow[:, 128 * k:128 * k + 128], ident[:], float(2 ** (7 - k)), A.mult, ["ident"], ["idpow"])
-        ts(T["ident256"][:], ident[:], 256.0, A.mult, ["ident"], ["ident256"])
-
-    def constants_last():
-        ts(T["qi"][:], T["qi"][:], 15, A.bitwise_and, ["qi"], ["qi"])
-        cp(T["qf"][:], T["qi"][:], ["qi"], ["qf"])
-        ts(T["dum"][:], T["qf"][:], float(NW), A.add, ["qf"], ["dum"])
-        ts(T["baseoff"][:], T["baseoff"][:], T["qf"][:, 0:1], A.add, ["qf", "baseoff"], ["baseoff"])
-        ts(T["cmpt"][:], T["cmpt"][:], T["qf"][:, 0:1], A.is_gt, ["qf", "cmpt"], ["cmpt"], s2=99999.0, o2=A.mult)
-        cp(T["shh"][:], T["shf"][:], ["shf"], ["shh"])
-
-    def header(t):
+            act(R("idpow", 128 * k, 128 * k + 128), R("ident"), FN.Copy, scale=float(2 ** (7 - k)))
+        ts(R("jc"), R("jc"), col("qf", 0), A.add)
+        ts(R("rti"), R("rti"), 15, A.bitwise_and)
+        ts(R("kge"), R("kge"), 8192.0, A.mult, -HALF, A.add)
+        ts(R("kc"), R("jc", 0, 128), 8192.0, A.mult, -HALF, A.add)
         for h in range(2):
-            mm(6, 256 * h, 256 * h + 256, ident[:], zin[t][:], True, True, ["ident", "z%d" % t])
-        if t > 0:
-            for b in MZV:
-                tt(mz[:, cols(b)], msk[t % 2][:, cols(b)], ps[6][:], A.mult, mb(t, b) + [("ps", 6)], [("mz", b)], [6])
+            ts(R("none", 16 * h, 16 * h + 16), R("jc", 0, 16), HALF + NW, A.add)
+        ts(R("mvb"), R("jc", 16, 128), 1.0 / 256, A.mult)
 
-    def masked(t):
-        for b in MZS:
-            mm(b, 0, 512, T["ident256"][:], msk[t % 2][:, cols(b)], True, False, ["ident256"] + mb(t, b))
-        for b in MZS:
-            for h in range(2):
-                mm(b, 256 * h, 256 * h + 256, ident[:], zin[t][:], False, h == 1, ["ident", "z%d" % t])
-        for b in MZS:
-            act(mz[:, cols(b)], ps[b][:], FN.Relu, [("ps", b), "m256"], [("mz", b)], [b], bias=T["m256"][:, 0:1])
+    def constants_write():
+        nb, first = len(BLOCKS), PAIRS[:PERIOD]
+        rows = [("ro", PERIOD, BLK, [o for c, o in first]), ("rc", PERIOD, BLK, [c for c, o in first]),
+                ("rs", BLK, 16 * PERIOD, [16 * first.index((c, c)) for c in range(BLK)]),
+                ("re", BLK + 1, 16 * PERIOD, [16 * first.index((c, 0)) + 15 for c in range(BLK)] + [0])]
+        chains = []
+        for name, period, step, values in rows:
+            chains.append([lambda name=name, period=period, step=step, i=i, v=v:
+                           ts(R(name, i, period * nb, period), R("cnt", 0, nb), float(step), A.mult, float(v), A.add)
+                           for i, v in enumerate(values)])
+        more = [lambda: ts(R("dg"), R("rti", 0, 32), 0.0, A.is_equal), lambda: tt(R("rtf"), R("rti"), R("blk"), A.add)]
+        for name, lo, n, most in (("ro", 0, 32, 15), ("rc", 32, 32, 15), ("rs", 64, 16, WD), ("re", 80, 32, WD - 1)):
+            more.append(lambda name=name, n=n, most=most: ts(R(name, 0, n), R(name, 0, n), float(most), A.min))
+        for name, lo, n in (("ro", 0, 32), ("rc", 32, 32), ("rs", 64, 16), ("re", 80, 32)):
+            more.append(lambda name=name, lo=lo, n=n: tt(R("row", lo, lo + n), R(name, 0, n), R("dg", 0, n), A.mult))
+        more += [lambda n=n: ts(R("inval", 16 * n, 16 * n + 16), R("cnt"), col("qf", 0), A.is_gt, 0.5, A.mult)
+                 for n, (c, o) in enumerate(PAIRS) if c == o]
+        more += [lambda j=j: op("V", V.tensor_reduce, ["out"], out=col("lf", j), in_=R("row", 16 * j, 16 * j + 16),
+                                axis=AxisListType.X, op=A.add) for j in range(7)]
+        more += [lambda: cp(R("lpair"), R("lf", 0, 4)), lambda: cp(col("lslot", 0), col("lf", 4)), lambda: cp(R("lend"), R("lf", 5, 7))]
+        turns = [lambda d=d: ts(R("rot", 128 * d, 128 * d + 128), R("rtf"), float(d), A.is_equal) for d in range(16)]
+        return chains, more, turns
 
-    def tolist(bank, c0, n, src, lo, hi, wt, rtags):
+    def tolist(out, src, lo, hi, wt, first=True):
         for q in range(16):
-            mm(bank, c0, c0 + n, T[wt][:, 16 - q:144 - q], src[:, lo + q:hi:16], q == 0, q == 15, [wt] + rtags)
+            mm(out, R(wt, 16 - q, 144 - q), R(src, lo + q, hi, 16), first and q == 0, q == 15)
 
-    def hashing(x, bank, n):
-        a, b, c = "hi%d" % x, "ha%d" % x, "hb%d" % x
-        hi, ha, hb = T[a], T[b], T[c]
-        return [lambda: cp(hi[:], ps[bank][:, 0:2 * n], [("ps", bank)], [a], [bank]),
-                lambda: ts(hi[:], hi[:], 4095, A.bitwise_and, [a], [a]),
-                lambda: tt(ha[:], hi[:, 0:n], hi[:, n:2 * n], A.mult, [a], [b]),
-                lambda: ts(hb[:], hi[:, 0:n], 37.0, A.mult, [a], [c]),
-                lambda: ts(ha[:], ha[:], 5, A.arith_shift_right, [b], [b]),
-                lambda: tt(ha[:], ha[:], hb[:], A.add, [b, c], [b])]
+    def hashing(src, hi, p, q, out, n):
+        return [lambda: cp(R(hi), src),
+                lambda: ts(R(hi), R(hi), 4095, A.bitwise_and),
+                lambda: tt(p, R(hi, 0, n), R(hi, n, 2 * n), A.mult),
+                lambda: ts(q, R(hi, 0, n), 37.0 * 32, A.mult, -HALF, A.add),
+                lambda: tt(p, p, q, A.add),
+                lambda: ts(out, p, 5, A.arith_shift_right, 4095, A.bitwise_and)]
 
     def places(h):
-        ha, tag, hu = T["ha%d" % h], "ha%d" % h, "hu%d" % h
-        return hashing(h, 4 + h, 64) + [lambda: ts(ha[:], ha[:], 4095, A.bitwise_and, [tag], [tag]),
-                                        lambda: cp(T[hu][:], ha[:], [tag], [hu])]
+        s = [R(n, 64 * h, 64 * h + 64) for n in ("hp", "hq", "hh", "hu", "base", "kc")]
+        return hashing(ps(4 + h, 0, 128), "hi%d" % h, s[0], s[1], s[2], 64) + [lambda: cp(s[3], s[2])]
 
-    def limits(t, b):
-        mm(SB[b], 0, 512, T["idm512"][:], msk[t % 2][:, cols(b)], True, False, ["idm512"] + mb(t, b))
-        mm(SB[b], 0, 512, T["id600"][:], T["ones"][:], False, True, ["id600", "ones"])
+    def sums(h):
+        tolist(ps(4 + h, 0, 64), "mz", 1024 * h, 1024 * h + 1024, "bigu")
+        tolist(ps(4 + h, 64, 128), "mz", 1024 * h, 1024 * h + 1024, "bigv")
 
-    def merge(first, second):
-        n = max(len(first), len(second))
-        for i in range(n):
-            for chain in (first, second):
-                for f in chain[i * len(chain) // n:(i + 1) * len(chain) // n]:
-                    f()
+    def before_probe(t, b):
+        if b in SG:
+            mm(ps(b), R("wipe"), bk(nbuf[t % 2], b), True, False)
+        mm(ps(b), R("nslope"), bk("mz", b), b not in SG, False)
 
-    def front(t, scatters):
-        for h in range(2):
-            rt = [("mz", 2 * h), ("mz", 2 * h + 1)]
-            tolist(4 + h, 0, 64, mz, 1024 * h, 1024 * h + 1024, "bigu", rt)
-            tolist(4 + h, 64, 64, mz, 1024 * h, 1024 * h + 1024, "bigv", rt)
-        if t == 0:
-            header(0)
-            constants_first()
-        for b in range(4):
-            if b not in SB:
-                mm(b, 0, 512, nident[:], mz[:, cols(b)], True, False, ["nident", ("mz", b)])
-        limits(t, 0)
-        merge([], scatters[:NSC])
-        merge(places(0) + places(1), scatters[NSC:])
-        if t == 0:
-            constants_mid()
-        limits(t, 2)
+    def before_none(t):
+        mm(ps(7, 0, 256), R("quart"), R("ones", 0, 256), True, False)
+        mm(ps(7, 0, 256), R("half"), R("zb%d" % t), False, False)
 
-    def gathermask(t, b):
-        h, o = b // 2, 32 * (b % 2)
-        hu = "hu%d" % h
-        win = tab[:, 0:NW].indirect(T[hu][:, o:o + 32])
-        if b in SB:
-            act(xh[:, cols(b)], win, FN.Copy, ["tab", hu], [("xh", b)])
+    def before_count(h):
+        mm(ps(4 + h, 0, 64), R("nbig"), R("lim"), True, False)
+
+    def gather(t, b):
+        win = G(R("tab", 0, NW), R("hu", 32 * b, 32 * b + 32))
+        if b in SG:
+            act(bk("xy", b), win, FN.Copy)
         else:
-            tt(yy[:, cols(b)], win, msk[t % 2][:, cols(b)], A.mult, ["tab", hu] + mb(t, b), [("yy", b)])
+            tt(bk("xy", b), win, bk(nbuf[t % 2], b), A.max)
 
     def difference(t, b):
-        if b in SB:
-            mm(b, 0, 512, ident[:], xh[:, cols(b)], True, False, ["ident", ("xh", b)])
-            for h in range(2):
-                mm(b, 256 * h, 256 * h + 256, nident[:], zin[t][:], False, h == 1, ["nident", "z%d" % t])
-        else:
-            mm(b, 0, 512, ident[:], yy[:, cols(b)], False, True, ["ident", ("yy", b)])
-
-    def absol(b):
-        act(ab[:, cols(b)], ps[b][:], FN.Abs, [("ps", b)], [("ab", b)], [b])
+        more = ([("nwipe", bk(nbuf[t % 2], b))] if b in SG else []) + ([("magic", R("ones"))] if b in FS else [])
+        more = [("slope", bk("xy", b))] + more
+        for i, (w, r) in enumerate(more):
+            mm(ps(b), R(w), r, False, i == len(more) - 1)
 
     def failing(b):
-        if b in SB:
-            tt(ff[:, cols(b)], ab[:, cols(b)], ps[SB[b]][:], A.is_gt, [("ab", b), ("ps", SB[b])], [("ff", b)], [SB[b]])
+        if b in FS:
+            act(bk("ff", b), ps(b), FN.Abs, bias=NMAGIC)
         else:
-            ts(ff[:, cols(b)], ab[:, cols(b)], float(LIMIT), A.is_gt, [("ab", b)], [("ff", b)])
+            ts(bk("ff", b), ps(b), MAGIC, A.add, MAGIC, A.not_equal)
 
     def prefix(b):
-        mm(b, 0, 512, T["triw"][:], ff[:, cols(b)], True, True, ["triw", ("ff", b)])
+        mm(ps(b), R("triw"), bk("ff", b), True, True)
 
     def firsts(b):
-        act(fr[:, cols(b)], ps[b][:], FN.Relu, [("ps", b)], [("fr", b)], [b], scale=-1.0)
+        act(bk("fr", b), ps(b), FN.Relu, scale=-1.0)
+
+    def weigh(b):
+        for k in (2 * b, 2 * b + 1):
+            mm(ps(4, 0, 256), R("idpow", 128 * k, 128 * k + 128), mk("fr", k), k == 0, k == NK - 1)
 
     def counts(h):
-        tolist(4 + h, 0, 64, ff, 1024 * h, 1024 * h + 1024, "sel", [("ff", 2 * h), ("ff", 2 * h + 1)])
+        tolist(ps(4 + h, 0, 64), "ff", 1024 * h, 1024 * h + 1024, "bigc", first=False)
 
-    def bases(h):
-        x = str(h)
-        tt(T["bs" + x][:], T["ha" + x][:], T["k4"][:, 64 * h:64 * h + 64], A.add, ["ha" + x, "k4"], ["bs" + x])
+    def keys(h, out):
+        tt(R("ky", 64 * h, 64 * h + 64), R("base", 64 * h, 64 * h + 64), ps(4 + h, 0, 64), A.max)
+        tt(out, R("ky", 64 * h, 64 * h + 32), R("ky", 64 * h + 32, 64 * h + 64), A.min)
 
-    def keys(h):
-        x = str(h)
-        ts(T["nk" + x][:], ps[4 + h][:, 0:64], T["lim"][:, 0:1], A.is_gt, [("ps", 4 + h), "lim"], ["nk" + x], [4 + h],
-           s2=32768.0, o2=A.mult)
-        tt(T["ky" + x][:], T["nk" + x][:], T["bs" + x][:], A.add, ["nk" + x, "bs" + x], ["ky" + x])
-        tt(T["ka" + x][:], T["ky" + x][:, 0:32], T["ky" + x][:, 32:64], A.min, ["ky" + x], ["ka" + x])
-        tt(T["kb" + x][:], T["ka" + x][:, 0:16], T["ka" + x][:, 16:32], A.min, ["ka" + x], ["kb" + x])
+    def merge(*chains):
+        for i in range(max(len(c) for c in chains)):
+            for c in chains:
+                if i < len(c):
+                    c[i]()
 
-    def moves(ks):
+    def thresholds(t, ks):
         for k in ks:
-            if k == NK:
-                ts(T["ob"][:, 112:128], T["jr"][:], 8.0, A.min, ["jr"], ["ob"], s2=256.0, o2=A.mult)
-            else:
-                ts(T["ob"][:, 16 * k - 16:16 * k], T["jr"][:], float(k), A.is_ge, ["jr"], ["ob"], s2=-256.0, o2=A.mult)
+            act(mk("th", k), mk(nbuf[t % 2], k), FN.Copy, scale=2.0 ** (8 - k) / OFF)
 
-    def scatter(t, c):
-        return lambda: cp(tab[:].indirect(T["scu"][:, 2 * c:2 * c + 1]), zin[t][:, 16 * c:16 * c + 16], ["scu", "z%d" % t], ["tab"])
+    constants_start()
+    ts(R("n0"), R("mini"), -OFF, A.mult, OFF, A.add)
+    for k in range(NK):
+        ts(mk("mz", k), R("zb0"), col("n0", k), A.max)
+        if k == 3:
+            ts(R("bigu"), R("sel"), col("wts", 0), A.mult)
+            ts(R("bigv"), R("sel"), col("wts", 1), A.mult)
+    for k in range(NK):
+        act(mk("na", k), R("ones", 0, 256), FN.Identity, scale=col("n0", k))
+    sums(0)
+    sums(1)
+    constants_key()
+    mm(ps(6, 0, 256), R("ident"), R("zb0"), True, True)
+    for b in range(4):
+        before_probe(0, b)
+    before_none(0)
+    chains, lists, more = constants_write()
+    merge(*chains)
+    merge(places(0), places(1), lists[:7])
+    merge(lists[7:])
+    thresholds(0, range(NK))
+    before_count(0)
+    before_count(1)
 
-    front(0, [])
     for t in range(STEPS):
-        zt, s2 = "z%d" % t, (t + 1) % 2
-        cur, nxt, ctags, ntags = msk[t % 2], msk[s2], mtags[t % 2], mtags[s2]
         last = t == STEPS - 1
+        cur, nxt, z, zn, zs = nbuf[t % 2], nbuf[(t + 1) % 2], R("zb%d" % t), "zb%d" % (t + 1), "zs%d" % (t + 1)
+
+        def moved(lo, hi):
+            return G(R(cur), R("mvu", 16 * lo - 16, 16 * hi - 16))
+
         for b in range(4):
-            gathermask(t, b)
-        if t == 0:
-            constants_last()
-        for b in range(4):
-            difference(t, b)
-            absol(b)
+            gather(t, b)
+        difference(t, 0)
+        difference(t, 1)
+        mm(ps(7, 0, 256), R("nhalf"), mk("xy", 0), False, False)
+        mm(ps(7, 0, 256), R("magic"), R("ones", 0, 256), False, True)
         failing(0)
-        prefix(0)
+        difference(t, 2)
+        difference(t, 3)
         failing(1)
-        counts(0)
-        bases(0)
-        bases(1)
-        prefix(1)
+        act(R("tab", NW, NW + NP), ps(7, 0, 256), FN.Identity, bias=NMAGIC)
         failing(2)
-        prefix(2)
+        tt(R("base"), R("hh"), R("kc"), A.add)
+        prefix(0)
+        counts(0)
         failing(3)
+        prefix(1)
+        firsts(0)
+        prefix(2)
         counts(1)
         prefix(3)
-        firsts(0)
         firsts(1)
+        keys(0, R("ka"))
+        tt(R("kb"), R("ka"), R("none"), A.min)
         firsts(2)
-        keys(0)
-        keys(1)
-        tt(T["key"][:], T["kb0"][:], T["kb1"][:], A.min, ["kb0", "kb1"], ["key"])
-        ts(T["nmu"][:], T["key"][:], 32768.0, A.is_ge, ["key"], ["nmu"])
-        ts(T["hs"][:], T["key"][:], 4095, A.bitwise_and, ["key"], ["hs"])
-        tt(T["sz"][:], T["sgn"][:].indirect(T["nmu"][:]), zin[t][:], A.mult, ["sgn", "nmu", zt], ["sz"])
-        cp(T["hsu"][:], T["hs"][:], ["hs"], ["hsu"])
-        act(T["cc"][:], T["ctab"][:].indirect(T["nmu"][:]), FN.Copy, ["ctab", "nmu"], ["cc"])
-        tt(T["yh"][:], tab[:, 0:NW].indirect(T["hsu"][:]), T["sz"][:], A.add, ["tab", "hsu", "sz"], ["yh"])
         firsts(3)
-        act(ps[7][:, 0:256], T["yh"][:], FN.Abs, ["yh"], [("ps", 7)], [7])
-        ts(T["jr"][:], T["key"][:], 12, A.arith_shift_right, ["key"], ["jr"])
+        keys(1, R("kc2"))
+        for b in range(4):
+            weigh(b)
+        tt(R("kd"), R("kc2"), R("kb"), A.min)
+        tt(R("key"), R("kd", 0, 16), R("kd", 16, 32), A.min)
+        act(R("ssb"), ps(4, 0, 256), FN.Copy)
+        ts(R("hs"), R("key"), 8191, A.bitwise_and)
+        ts(R("ju"), R("key"), 1.0 / 8192, A.mult, 1024.0, A.add)
+        cp(R("hsu"), R("hs"))
         if not last:
-            ts(T["nmf"][:], T["key"][:], 32768.0, A.is_ge, ["key"], ["nmf"])
-        cp(T["jru"][:], T["jr"][:], ["jr"], ["jru"])
-        act(T["thr"][:], T["thrt"][:].indirect(T["jru"][:]), FN.Copy, ["thrt", "jru"], ["thr"])
-        moves(range(1, 1 + NOB))
-        tt(T["wh"][:], T["cc"][:], ps[7][:, 0:256], A.mult, ["cc", ("ps", 7)], ["wh"], [7])
-        ts(nz[t][:], T["wh"][:], MAGIC, A.add, ["wh"], [("nz", t)], s2=-MAGIC, o2=A.add)
+            ts(R("nm"), R("key"), HALF, A.is_ge)
+        tt(R("dz%d" % t), G(R("tab"), R("hsu")), z, A.subtract)
         if not last:
             rid, pid = topo.addr(nxt_core, core)
-            hold("G", [("nz", t)], [], ())
-            g.remote_dma(out_ap=zin[t + 1][:], in_ap=nz[t][:], remote_sem=T.sem["arr%d" % (t + 1)], local_sem=T.sem["sent"],
+            hold("G", [R("dz%d" % t)], [])
+            g.remote_dma(out_ap=ap(R(zs)), in_ap=ap(R("dz%d" % t)), remote_sem=T.sem["arr%d" % (t + 1)], local_sem=T.sem["sent"],
                          pid=pid, routing_id=rid, dma_engine_mask=topo.mask(core, nxt_core))
-            lastw["z%d" % (t + 1)] = ("arr%d" % (t + 1), len(topo.engines(prv_core, core)))
-        dma("Y", g.sync.dma_start, "outs", 16 * (t + 1), [("nz", t)], [], out=T["yz"][:, NP * t:NP * t + NP], in_=nz[t][:])
-        moves(range(1 + NOB, 9))
-        tt(T["of"][:], T["ob"][:], T["baseoff"][:], A.add, ["ob", "baseoff"], ["of"])
-        if not last:
-            mm(4, 256, 272, T["ones"][:, 0:128], T["nmf"][:], True, True, ["ones", "nmf"])
-        for k in range(NK):
-            mm(4, 0, 256, idpow[:, 128 * k:128 * k + 128], fr[:, 256 * k:256 * k + 256], k == 0, k == NK - 1,
-               ["idpow", ("fr", k // 2)])
-        tt(T["u1"][:], T["thr"][:], ps[4][:, 0:256], A.is_le, ["thr", ("ps", 4)], ["u1"], [4])
-        cp(T["offu"][:], T["of"][:], ["of"], ["offu"])
-        low = cur[:].indirect(T["offu"][:, 0:48])
-        if not last:
-            act(nxt[:, 256:1024], low, FN.Copy, ctags + ["offu"], ntags[1:4])
-        act(nxt[:, 1024:2048], cur[:].indirect(T["offu"][:, 48:112]), FN.Copy, ctags + ["offu"], ntags[4:8])
-        tt(nxt[:, 0:256], cur[:].indirect(T["offu"][:, 112:128]), T["u1"][:], A.max, ctags + ["offu", "u1"], [ntags[0]])
+            note("arr%d" % (t + 1), len(topo.engines(prv_core, core)), [], [R(zs)])
+        tt(R("ub"), G(R("th"), R("ju")), R("ssb"), A.is_le)
+        tt(R("ge"), G(R("key"), R("lrep", 0, 7)), R("kge"), A.is_ge)
         if last:
-            cp(nxt[:, 256:1024], low, ctags + ["offu"], ntags[1:4])
+            tt(R("mv"), R("mvb"), R("ge"), A.subtract)
+            ts(R("mvu"), R("mv"), 256.0, A.mult)
+            store(T["ym"][:, 0:256], R("ub"))
+            for lo, hi in ((1, 3), (3, 5), (5, 7), (7, 8)):
+                src = G(R(cur), R("mvu", 16 * lo - 16, 16 * hi - 16))
+                if lo in (1, 5):
+                    act(R("mo", 256 * lo, 256 * hi), src, FN.Relu, scale=-1.0, bias=ONE)
+                else:
+                    ts(R("mo", 256 * lo, 256 * hi), src, 1.0, A.is_lt)
+                store(T["ym"][:, 256 * lo:256 * hi], R("mo", 256 * lo, 256 * hi))
+            act(R("nz%d" % t), R("dz%d" % t), FN.Abs)
+            store(T["yz"][:, NP * t:NP * t + NP], R("nz%d" % t))
             break
-        tt(T["uz"][:], nxt[:, 0:256], ps[6][:, 0:256], A.mult, [ntags[0], ("ps", 6)], ["uz"], [6])
-        tolist(5, 0, 16, T["uz"], 0, 256, "bigu", ["uz"])
-        tolist(5, 16, 16, T["uz"], 0, 256, "bigv", ["uz"])
-        op("V", V.tensor_reduce, [("ps", 4)], ["asum"], [4], out=T["asum"][:], in_=ps[4][:, 256:272], axis=AxisListType.X, op=A.add)
-        cp(T["ai"][:, 0:1], T["asum"][:], ["asum"], ["ai"])
-        ts(T["ai"][:, 0:1], T["ai"][:, 0:1], 1, A.bitwise_and, ["ai"], ["ai"])
-        ts(T["lim"][:, 0:1], T["ai"][:, 0:1], 1.5, A.add, ["ai"], ["lim"])
-        for f in hashing(2, 5, 16):
-            f()
-        ts(T["pl"][:], T["ha2"][:], 4095, A.bitwise_and, ["ha2"], ["pl"])
-        ts(T["hlb"][:], T["pl"][:], -2048.0, A.add, ["pl"], ["hlb"])
-        header(t + 1)
-        for d in range(15):
-            mm(7, 16 * d, 16 * d + 16, T["shh"][:, 128 * d:128 * d + 128], T["hlb"][:], True, True, ["shh", "hlb"])
-        masked(t + 1)
-        tt(T["eq"][:], T["cmpt"][:], ps[7][:, 0:240], A.is_equal, ["cmpt", ("ps", 7)], ["eq"], [7])
-        for d in range(15):
-            mm(5, 32, 48, ident[:], T["eq"][:, 16 * d:16 * d + 16], d == 0, d == 14, ["ident", "eq"])
-        ts(T["lo"][:], ps[5][:, 32:48], 0.5, A.is_gt, [("ps", 5), "dum"], ["lo"], [5], s2=T["dum"][:, 0:1], o2=A.mult)
-        tt(T["so"][:], T["lo"][:], T["pl"][:], A.max, ["lo", "pl"], ["so"])
-        cp(T["scu"][:, 0:32:2], T["so"][:], ["so"], ["scu"])
-        front(t + 1, [scatter(t, c) for c in range(15, -1, -1)])
-    s2 = STEPS % 2
-    n = 16 * STEPS
-    for lo, hi, tags in ((0, 256, mtags[s2][0:1]), (256, 1024, mtags[s2][1:4]), (1024, 2048, mtags[s2][4:8])):
-        n += 16
-        dma("Y", g.sync.dma_start, "outs", n, tags, [], out=T["ym"][:, lo:hi], in_=msk[s2][:, lo:hi])
-    g.sync.wait_ge(T.sem["outs"], n)
-    for e in ("V", "S", "P", "G"):
+        tt(R("uz"), R("ub"), ps(6, 0, 256), A.mult)
+        tt(R("mv"), R("mvb"), R("ge"), A.subtract)
+        ts(R("mvu"), R("mv"), 256.0, A.mult)
+        tolist(ps(5, 0, 16), "uz", 0, 256, "bigu")
+        tolist(ps(5, 16, 32), "uz", 0, 256, "bigv")
+        mm(ps(4, 0, 16), R("ones", 0, 128), R("nm"), True, True)
+        act(mk(nxt, 0), R("ub"), FN.Identity, scale=-OFF, bias=POFF)
+        cp(bk(nxt, 1), moved(2, 4))
+        for lo, hi in ((1, 2), (4, 6), (6, 8)):
+            act(R(nxt, 256 * lo, 256 * hi), moved(lo, hi), FN.Copy)
+        act(R("par"), ps(4, 0, 16), FN.Identity, scale=0.5, bias=M64, accum_out=col("px", 0))
+        parity = [lambda: act(col("px", 1), col("px", 0), FN.Identity, bias=PMAGIC),
+                  lambda: act(col("px", 2), col("px", 1), FN.Identity, bias=NMAGIC),
+                  lambda: act(col("px", 3), col("px", 2), FN.Identity, scale=-1.0, bias=col("px", 0)),
+                  lambda: act(R("lim"), R("two"), FN.Identity, scale=col("px", 3), bias=P175)]
+        mm(ps(7, 0, WD), R("ident"), R("inval"), True, False)
+        for b in SG:
+            mm(ps(b), R("neg"), bk(nxt, b), True, False)
+        merge(hashing(ps(5, 0, 32), "hi2", R("gp"), R("gq"), R("pl"), 16), *[more[i::4] for i in range(4)])
+        more = []
+        ts(R("hx"), G(R("pl"), R("lpair")), -2048.0, A.add)
+        cp(G(R("clamp"), col("lslot", 0)), R("pl"))
+        for d in range(16):
+            mm(ps(7, d, WD, 16), R("rot", 128 * d, 128 * d + 128), R("hx", 0, NPAIR), False, False)
+        act(R(zn), R(zs), FN.Abs)
+        act(ps(6, 0, 256), R(zs), FN.Abs)
+        for b in SG:
+            for h in range(2):
+                mm(ps(b, 256 * h, 256 * h + 256), R("ident"), R(zn), False, h == 1)
+        for d in range(16):
+            mm(ps(7, d, WD, 16), R("nid"), R("hx", 32, 32 + NPAIR), False, d == 15)
+        for b in SG:
+            act(bk("mz", b), ps(b), FN.Relu)
+        for k in range(NK):
+            if k // 2 not in SG:
+                tt(mk("mz", k), mk(nxt, k), ps(6, 0, 256), A.max)
+        ts(R("eq"), ps(7, 0, WD), 0.0, A.is_equal, 8192.0, A.mult)
+        sums(0)
+        sums(1)
+        op("V", V.tensor_tensor_scan, ["out"], out=R("st"), data0=R("eq"), data1=R("clamp", 0, WD), initial=0.0, op0=A.add,
+           op1=A.min)
+        merge(parity, [lambda k=k: thresholds(t + 1, [k]) for k in range(NK)])
+        act(R("nz%d" % t), R("dz%d" % t), FN.Abs)
+        store(T["yz"][:, NP * t:NP * t + NP], R("nz%d" % t))
+        for b in range(4):
+            before_probe(t + 1, b)
+        before_none(t + 1)
+        scatters = [lambda m=m, blk=blk: cp(G(R("tab"), R("scu", 4 * m, 4 * m + len(blk))),
+                                            R("zb%d" % t, 16 * blk[0], 16 * blk[-1] + 16)) for m, blk in enumerate(BLOCKS)][::-1]
+        h0, h1 = places(0), places(1)
+        cp(R("scu"), G(R("st"), R("lend")))
+        merge(h0[:3], scatters[:3])
+        merge(h1[:3], h0[3:6], scatters[3:])
+        merge(h1[3:], h0[6:])
+        before_count(0)
+        before_count(1)
+    g.sync.wait_ge(T.sem["outs"], stored[0])
+    for e in QUEUES:
         g.sync.wait_ge(T.sem[semof[e]], count[e])
     g.wait_ge(T.sem["sent"], (STEPS - 1) * len(topo.engines(core, nxt_core)))

@@ -5,47 +5,54 @@ A = AluOpType
 FN = ActivationFunctionType
 STEPS, NP, NK, NW = 6, 256, 8, 4096
 MAGIC = 12582912.0
+ROUND = MAGIC * 4096
+CENTRE = 4096.0 * 2040
 SLOPE = 185.0 / 32768
 OFF = 4096.0
-WIPE = 2.0 ** 22
+WIPE = 9 * MAGIC / OFF
 BIG = 2.0 ** 25
 HALF = 2.0 ** 23
+TOP = 8192.0
 B16, F32, I32, U16, F16 = "bfloat16", "float32", "int32", "uint16", "float16"
 SG = (0, 2)
-FS = (2,)
+SM = (0, 2)
+MOVES = ((1, 2), (2, 4), (4, 6), (6, 8))
+VMOVE = (1,)
+FB = 6
+PROBE = "g1 d1 g0 g3 d0 d3 g2 f0 d2 f2 f1 q0 c0 none ncol f3 q1 q2 y0 k0 kb c1 y1 k1 kd key r0 hs r1 ju hsu r2 r3 ssb stay"
+WRITE = "ge down dz mvu q3 ub q4 uz nm send m0 su sv inval m1 q5 w0 q6 w1 q7 w3 code m2 n2 m3 t4 w2 q8 w4 n0 t7 zps z2 p0 x2 w5 z0 x0 hx others v7 p1 v6 own e1 e0 v2 npl presum v3 sums b3 slot p2 a1 u1 b1 a0 h0 h2 s5 t1 p3 t2 t3 u0 t5 s4 h1 prenone s3 b0 h3 h4 s2 p4 h5 h6 s1 h7 t6 h9 h8 l0 t0 l1 prefirst b2 s0"
+LAST = "ge dz down send mvu ub out o0 o1 o2 o3"
 BLK = 3
 BLOCKS = [list(range(c, min(c + BLK, 16))) for c in range(0, 16, BLK)]
 PAIRS = [(c, o) for blk in BLOCKS for c in blk for o in range(c, blk[0] - 1, -1)]
 NPAIR = len(PAIRS)
 WD = 16 * NPAIR
 PERIOD = BLK * (BLK + 1) // 2
+CUT = 16 * PERIOD * 4
 
 _SB = {
     "tab": (NW + NP, B16), "na": (2048, B16), "nb": (2048, B16), "th": (2064, B16), "mz": (2048, B16), "xy": (2048, B16),
-    "ff": (2048, B16), "fr": (2048, B16), "mini": (8, B16), "wts": (2, B16), "ones": (512, B16), "n0": (8, F32), "th0": (8, F32),
-    "ident": (128, B16), "slope": (128, B16), "nslope": (128, B16), "wipe": (128, B16), "nwipe": (128, B16), "half": (128, B16),
-    "nhalf": (128, B16), "quart": (128, B16), "magic": (128, B16), "nbig": (128, B16), "idpow": (1024, B16), "triw": (128, B16),
-    "sel": (144, B16), "bigu": (144, B16), "bigv": (144, B16), "bigc": (144, B16), "blk": (128, B16), "neg": (128, B16),
-    "rot": (2048, F16), "nid": (128, F16), "rti": (128, I32), "rtf": (128, F32), "inval": (WD, B16), "clamp": (16 * PERIOD * len(BLOCKS), F32),
-    "qi": (8, I32), "qf": (8, F32), "cb": (8, F32), "jc": (144, F32), "kc": (128, F32), "kge": (112, F32), "mvb": (112, F32),
-    "none": (32, F32), "tmp": (16, F32), "row": (128, F32), "lrep": (8, U16), "lpair": (4, U16), "lslot": (2, U16), "lend": (2, U16),
-    "hi0": (128, I32), "hi1": (128, I32), "hi2": (32, I32), "hp": (128, I32), "hq": (128, I32), "hh": (128, I32), "hu": (128, U16),
-    "gp": (16, I32), "gq": (16, I32), "pl": (16, I32), "base": (128, F32), "ky": (128, F32), "ka": (32, F32), "kb": (32, F32),
-    "kc2": (32, F32), "kd": (32, F32), "key": (16, I32), "hs": (16, I32), "hsu": (16, U16), "ju": (16, U16), "nm": (16, B16),
-    "ge": (112, F32), "mv": (112, F32), "mvu": (112, U16), "ssb": (256, B16), "ub": (256, B16), "uz": (256, B16),
+    "ff": (2048, B16), "tri": (1024, B16), "nmag": (256, B16), "c128": (256, B16), "mini": (8, B16), "wts": (2, B16),
+    "ones": (256, B16), "n0": (8, F32), "ident": (128, B16), "slope": (128, B16), "nslope": (128, B16), "wipe": (128, B16),
+    "unwipe": (512, B16), "nhalf": (128, B16), "magic": (128, B16), "nbig": (128, B16), "pow": (11 * 128, B16),
+    "neg": (128, B16), "round": (128, B16), "p8192": (128, B16), "sums": (256, B16),
+    "sel": (144, B16), "bigu": (144, B16), "bigv": (144, B16), "bigc": (144, B16), "blk": (128, B16), "uv": (16, B16),
+    "nuv": (16, B16), "rot": (2048, F16), "nid": (128, F16), "rti": (144, I32), "rtf": (128, B16), "inval": (WD, B16),
+    "clamp": (16 * PERIOD * len(BLOCKS), F32), "qi": (8, I32), "qf": (8, F32), "jc": (128, B16), "kq": (1, F32),
+    "kge": (128, F32), "none": (32, F32), "row": (144, F32), "lrep": (8, U16), "lst": (10, U16),
+    "hu": (128, F32), "hq": (128, F32), "hs1": (128, I32), "hh": (128, I32), "h16": (128, F16), "hl": (128, U16),
+    "hi2": (32, I32), "gp": (16, I32), "gq": (16, I32), "pl": (16, I32), "npl": (16, F32), "base": (128, F32), "ky": (128, F32),
+    "ka": (32, F32), "kb": (32, F32), "kc": (32, F32), "kd": (32, F32), "key": (16, I32), "hs": (16, I32), "hsu": (16, U16),
+    "ju": (16, U16), "ge": (128, B16), "mvu": (112, U16), "ssb": (256, B16), "ub": (256, B16), "uz": (256, B16), "dz": (256, B16),
     "hx": (64, F16), "eq": (WD, B16), "st": (WD, F32), "scu": (32, U16), "par": (16, F32), "px": (8, F32), "lim": (64, B16),
-    "two": (64, B16), "mo": (2048, B16), "cnt": (16, F32), "dg": (32, F32), "lf": (8, F32),
-    "ro": (36, F32), "rc": (36, F32), "rs": (18, F32), "re": (32, F32),
+    "mo": (2048, B16), "cnt": (144, F32), "dg": (144, F32),
 }
 SCRATCH = {}
 for _n in _SB:
     SCRATCH[_n] = ("sbuf", [128, _SB[_n][0]], _SB[_n][1])
 for _t in range(STEPS):
     SCRATCH["zb%d" % _t] = ("sbuf", [128, NP], B16)
-    SCRATCH["dz%d" % _t] = ("sbuf", [128, NP], B16)
     SCRATCH["nz%d" % _t] = ("sbuf", [128, NP], B16)
-    if _t:
-        SCRATCH["zs%d" % _t] = ("sbuf", [128, NP], B16)
 for _b in range(8):
     SCRATCH["ps%d" % _b] = ("psum", [128, 512], F32)
 
@@ -110,13 +117,16 @@ def rank_program(g, core, T, topo):
                     marks_of[f] = np.zeros(SCRATCH[r[0]][1][1], np.int64)
                 marks_of[f][r[1]:r[2]] = n
 
-    def op(e, call, outs, **kw):
+    def op(e, call, outs, row=None, **kw):
         wr = [kw[k] for k in outs]
         rd = [v for k, v in kw.items() if isinstance(v, tuple) and k not in outs]
         rd += [r[4] for r in rd + wr if len(r) > 4]
         hold(e, rd, wr)
         count[e] += 1
-        call(**{k: ap(v) if isinstance(v, tuple) else v for k, v in kw.items()}).then_inc(T.sem[semof[e]], 1)
+        args = {k: ap(v) if isinstance(v, tuple) else v for k, v in kw.items()}
+        if row is not None:
+            args[outs[0]] = T[wr[0][0]][row:row + 1, wr[0][1]:wr[0][2]]
+        call(**args).then_inc(T.sem[semof[e]], 1)
         snap[(e, count[e])] = dict(known[e])
         note(e, count[e], rd, wr)
 
@@ -147,11 +157,11 @@ def rank_program(g, core, T, topo):
     def mm(out, lhsT, rhs, start, stop):
         op("P", P.matmul, ["out"], out=out, lhsT=lhsT, rhs=rhs, start=start, stop=stop)
 
-    def fill(r, val):
-        op("V", V.memset, ["ap"], ap=r, constant=val)
+    def fill(r, val, row=None):
+        op("V", V.memset, ["ap"], row, ap=r, constant=val)
 
-    def select(n, pattern, cmp, val, base, mul):
-        op("G", g.affine_select, ["out"], out=R(n), in_=R(n), pattern=pattern, compare_op=cmp, fill=val, base=base,
+    def select(r, pattern, cmp, val, base, mul):
+        op("G", g.affine_select, ["out"], out=r, in_=r, pattern=pattern, compare_op=cmp, fill=val, base=base,
            channel_multiplier=mul)
 
     def iota(r, pattern, base, mul):
@@ -170,306 +180,323 @@ def rank_program(g, core, T, topo):
     def col(name, j):
         return R(name, j, j + 1)
 
-    nbuf = ["na", "nb"]
-    NMAGIC, POFF, ONE, P175, M64, PMAGIC = (col("cb", j) for j in range(6))
-
-    load(g.sync, "ldz", R("zb0"), T["z0"][:])
-    load(g.scalar, "ldm", R("mini"), T["m0"][:])
-    load(g.sync, "ldw", R("wts"), T["wt"][:])
-    load(g.scalar, "ldx", R("tab", 0, NW), T["xr"][:])
-
-    def constants_start():
-        for n in ("sel", "ident", "triw", "ones"):
-            fill(R(n), 1.0)
-        for n in ("blk", "inval", "re"):
-            fill(R(n), 0.0)
-        for j, v in enumerate((-MAGIC, OFF, 1.0, 1.75, -1.0 / 64, MAGIC)):
-            fill(col("cb", j), v)
-        fill(R("lim"), 1.25)
-        fill(R("th", 2048, 2064), 1.0)
-        fill(R("two"), 2.0)
-        select("ident", [[1, 128]], A.is_equal, 0.0, 0, -1)
-        select("sel", [[-16, 9], [-1000, 16]], A.is_ge, 0.0, 16, 1)
-        iota(R("qi"), [[0, 8]], 0, 1)
-        select("sel", [[16, 9], [-1000, 16]], A.is_ge, 0.0, -1, -1)
-        iota(R("jc"), [[256, 9], [16, 16]], 0, 0)
-        select("blk", [[-16, 8], [0, 16]], A.is_ge, 100.0, 0, 1)
-        iota(R("cnt"), [[1, 16]], 0, 0)
-        select("blk", [[16, 8], [0, 16]], A.is_ge, 100.0, 15, -1)
-        iota(R("rti"), [[1, 128]], 128, -1)
-        select("triw", [[-16, 8], [0, 16]], A.is_ge, 0.0, 0, 1)
-        iota(R("kge"), [[256, 7], [0, 16]], 256, 0)
-        select("triw", [[1, 128]], A.is_ge, 0.0, -1, -1)
-        iota(R("clamp"), [[0, len(BLOCKS)], [-16, PERIOD], [0, 16]], NW + 16 * (PERIOD - 1), 1)
-        select("triw", [[1, 128]], A.not_equal, -1.0, 0, -1)
-        for n, v in (("wipe", WIPE), ("nslope", -SLOPE), ("slope", SLOPE), ("nwipe", -WIPE), ("nbig", -BIG), ("half", 0.5),
-                     ("quart", 0.25), ("nhalf", -0.5), ("magic", MAGIC), ("neg", -1.0)):
-            act(R(n), R("ident"), FN.Copy, scale=v)
-        ts(R("qi"), R("qi"), 15, A.bitwise_and)
-        ts(R("nid"), R("ident"), -1.0, A.mult)
-        cp(R("qf"), R("qi"))
-        cp(R("lrep"), R("qi"))
-
-    def constants_key():
-        ts(R("bigc"), R("sel"), BIG, A.mult)
-        for k in range(NK):
-            act(R("idpow", 128 * k, 128 * k + 128), R("ident"), FN.Copy, scale=float(2 ** (7 - k)))
-        ts(R("jc"), R("jc"), col("qf", 0), A.add)
-        ts(R("rti"), R("rti"), 15, A.bitwise_and)
-        ts(R("kge"), R("kge"), 8192.0, A.mult, -HALF, A.add)
-        ts(R("kc"), R("jc", 0, 128), 8192.0, A.mult, -HALF, A.add)
-        for h in range(2):
-            ts(R("none", 16 * h, 16 * h + 16), R("jc", 0, 16), HALF + NW, A.add)
-        ts(R("mvb"), R("jc", 16, 128), 1.0 / 256, A.mult)
-
-    def constants_write():
-        nb, first = len(BLOCKS), PAIRS[:PERIOD]
-        rows = [("ro", PERIOD, BLK, [o for c, o in first]), ("rc", PERIOD, BLK, [c for c, o in first]),
-                ("rs", BLK, 16 * PERIOD, [16 * first.index((c, c)) for c in range(BLK)]),
-                ("re", BLK + 1, 16 * PERIOD, [16 * first.index((c, 0)) + 15 for c in range(BLK)] + [0])]
-        chains = []
-        for name, period, step, values in rows:
-            chains.append([lambda name=name, period=period, step=step, i=i, v=v:
-                           ts(R(name, i, period * nb, period), R("cnt", 0, nb), float(step), A.mult, float(v), A.add)
-                           for i, v in enumerate(values)])
-        more = [lambda: ts(R("dg"), R("rti", 0, 32), 0.0, A.is_equal), lambda: tt(R("rtf"), R("rti"), R("blk"), A.add)]
-        for name, lo, n, most in (("ro", 0, 32, 15), ("rc", 32, 32, 15), ("rs", 64, 16, WD), ("re", 80, 32, WD - 1)):
-            more.append(lambda name=name, n=n, most=most: ts(R(name, 0, n), R(name, 0, n), float(most), A.min))
-        for name, lo, n in (("ro", 0, 32), ("rc", 32, 32), ("rs", 64, 16), ("re", 80, 32)):
-            more.append(lambda name=name, lo=lo, n=n: tt(R("row", lo, lo + n), R(name, 0, n), R("dg", 0, n), A.mult))
-        more += [lambda n=n: ts(R("inval", 16 * n, 16 * n + 16), R("cnt"), col("qf", 0), A.is_gt, 0.5, A.mult)
-                 for n, (c, o) in enumerate(PAIRS) if c == o]
-        more += [lambda j=j: op("V", V.tensor_reduce, ["out"], out=col("lf", j), in_=R("row", 16 * j, 16 * j + 16),
-                                axis=AxisListType.X, op=A.add) for j in range(7)]
-        more += [lambda: cp(R("lpair"), R("lf", 0, 4)), lambda: cp(col("lslot", 0), col("lf", 4)), lambda: cp(R("lend"), R("lf", 5, 7))]
-        turns = [lambda d=d: ts(R("rot", 128 * d, 128 * d + 128), R("rtf"), float(d), A.is_equal) for d in range(16)]
-        return chains, more, turns
-
-    def tolist(out, src, lo, hi, wt, first=True):
-        for q in range(16):
-            mm(out, R(wt, 16 - q, 144 - q), R(src, lo + q, hi, 16), first and q == 0, q == 15)
-
-    def hashing(src, hi, p, q, out, n):
-        return [lambda: cp(R(hi), src),
-                lambda: ts(R(hi), R(hi), 4095, A.bitwise_and),
-                lambda: tt(p, R(hi, 0, n), R(hi, n, 2 * n), A.mult),
-                lambda: ts(q, R(hi, 0, n), 37.0 * 32, A.mult, -HALF, A.add),
-                lambda: tt(p, p, q, A.add),
-                lambda: ts(out, p, 5, A.arith_shift_right, 4095, A.bitwise_and)]
-
-    def places(h):
-        s = [R(n, 64 * h, 64 * h + 64) for n in ("hp", "hq", "hh", "hu", "base", "kc")]
-        return hashing(ps(4 + h, 0, 128), "hi%d" % h, s[0], s[1], s[2], 64) + [lambda: cp(s[3], s[2])]
-
-    def sums(h):
-        tolist(ps(4 + h, 0, 64), "mz", 1024 * h, 1024 * h + 1024, "bigu")
-        tolist(ps(4 + h, 64, 128), "mz", 1024 * h, 1024 * h + 1024, "bigv")
-
-    def before_probe(t, b):
-        if b in SG:
-            mm(ps(b), R("wipe"), bk(nbuf[t % 2], b), True, False)
-        mm(ps(b), R("nslope"), bk("mz", b), b not in SG, False)
-
-    def before_none(t):
-        mm(ps(7, 0, 256), R("quart"), R("ones", 0, 256), True, False)
-        mm(ps(7, 0, 256), R("half"), R("zb%d" % t), False, False)
-
-    def before_count(h):
-        mm(ps(4 + h, 0, 64), R("nbig"), R("lim"), True, False)
-
-    def gather(t, b):
-        win = G(R("tab", 0, NW), R("hu", 32 * b, 32 * b + 32))
-        if b in SG:
-            act(bk("xy", b), win, FN.Copy)
-        else:
-            tt(bk("xy", b), win, bk(nbuf[t % 2], b), A.max)
-
-    def difference(t, b):
-        more = ([("nwipe", bk(nbuf[t % 2], b))] if b in SG else []) + ([("magic", R("ones"))] if b in FS else [])
-        more = [("slope", bk("xy", b))] + more
-        for i, (w, r) in enumerate(more):
-            mm(ps(b), R(w), r, False, i == len(more) - 1)
-
-    def failing(b):
-        if b in FS:
-            act(bk("ff", b), ps(b), FN.Abs, bias=NMAGIC)
-        else:
-            ts(bk("ff", b), ps(b), MAGIC, A.add, MAGIC, A.not_equal)
-
-    def prefix(b):
-        mm(ps(b), R("triw"), bk("ff", b), True, True)
-
-    def firsts(b):
-        act(bk("fr", b), ps(b), FN.Relu, scale=-1.0)
-
-    def weigh(b):
-        for k in (2 * b, 2 * b + 1):
-            mm(ps(4, 0, 256), R("idpow", 128 * k, 128 * k + 128), mk("fr", k), k == 0, k == NK - 1)
-
-    def counts(h):
-        tolist(ps(4 + h, 0, 64), "ff", 1024 * h, 1024 * h + 1024, "bigc", first=False)
-
-    def keys(h, out):
-        tt(R("ky", 64 * h, 64 * h + 64), R("base", 64 * h, 64 * h + 64), ps(4 + h, 0, 64), A.max)
-        tt(out, R("ky", 64 * h, 64 * h + 32), R("ky", 64 * h + 32, 64 * h + 64), A.min)
-
     def merge(*chains):
         for i in range(max(len(c) for c in chains)):
             for c in chains:
                 if i < len(c):
                     c[i]()
 
-    def thresholds(t, ks):
-        for k in ks:
-            act(mk("th", k), mk(nbuf[t % 2], k), FN.Copy, scale=2.0 ** (8 - k) / OFF)
+    nbuf = ["na", "nb"]
+    NMAGIC, POFF, ONE, M64, PMAGIC, NHALF = -MAGIC, OFF, 1.0, -1.0 / 64, MAGIC, -HALF
 
-    constants_start()
+    load(g.sync, "ldz", R("zb0"), T["z0"][:])
+    load(g.scalar, "ldm", R("mini"), T["m0"][:])
+    load(g.sync, "ldw", R("wts"), T["wt"][:])
+    load(g.scalar, "ldx", R("tab", 0, NW), T["xr"][:])
+
+    def halving(name):
+        n, calls = 128, []
+        while n < SCRATCH[name][1][1]:
+            m = min(n, SCRATCH[name][1][1] - n)
+            calls.append(lambda n=n, m=m: ts(R(name, n, n + m), R(name, 0, m), 2.0 ** -(n // 128), A.mult))
+            n += m
+        return calls
+
+    def periodic(lo, values, period):
+        for i in range(min(period, len(values))):
+            v = values[i::period]
+            iota(R("row", lo + i, lo + i + period * (len(v) - 1) + 1, period), [[v[1] - v[0] if len(v) > 1 else 0, len(v)]], v[0], 0)
+
+    fill(R("ident"), 1.0)
+    fill(R("sel"), 1.0)
+    select(R("ident"), [[1, 128]], A.is_equal, 0.0, 0, -1)
+    fill(R("sums"), 0.0)
+    fill(R("tri", 0, 128), 128.0 / 32)
+    fill(R("blk"), 0.0)
+    merge([lambda row=row, v=v: fill(R("sums", 0, 128), v, row) for row, v in ((0, -HALF), (32, HALF - CENTRE - 2048), (64, 0.5))],
+          [lambda row=row, v=v: fill(R("sums", 128, 256), v, row) for row, v in ((0, -ROUND), (32, CENTRE))],
+          [lambda n=n, v=v: fill(R(n), v) for n, v in (("ones", 1.0), ("row", 0.0), ("inval", 0.0), ("nmag", -MAGIC),
+                                                       ("c128", 128.0), ("lim", 80.0))])
+    fill(R("th", 2048, 2064), 1.0)
+    select(R("sel"), [[-16, 9], [-1000, 16]], A.is_ge, 0.0, 16, 1)
+    iota(R("qi"), [[0, 8]], 0, 1)
+    select(R("sel"), [[16, 9], [-1000, 16]], A.is_ge, 0.0, -1, -1)
+    iota(R("jc"), [[256, 8], [16, 16]], 0, 0)
+    select(R("tri", 0, 128), [[-16, 8], [0, 16]], A.is_ge, 0.0, 0, 1)
+    iota(R("kge"), [[256, 8], [0, 16]], 256, 0)
+    select(R("tri", 0, 128), [[1, 128]], A.is_ge, 0.0, -1, -1)
+    iota(R("cnt"), [[0, 9], [1, 16]], 0, 0)
+    select(R("tri", 0, 128), [[1, 128]], A.not_equal, -128.0 * 33 / 64, 0, -1)
+    iota(R("rti"), [[1, 144]], 128, -1)
+    select(R("blk"), [[-16, 8], [0, 16]], A.is_ge, 100.0, 0, 1)
+    iota(R("clamp"), [[0, len(BLOCKS)], [16, PERIOD], [0, 16]], int(TOP) - NW - 16 * (PERIOD - 1), -1)
+    select(R("blk"), [[16, 8], [0, 16]], A.is_ge, 100.0, 15, -1)
+    ends = [[16 * PAIRS.index((c, blk[0])) + 15 for c in blk] + [0] * (BLK + 1 - len(blk)) for blk in BLOCKS]
+    periodic(0, [o for c, o in PAIRS], PERIOD)
+    periodic(32, [c for c, o in PAIRS], PERIOD)
+    periodic(64, [16 * PAIRS.index((c, c)) for c in range(16)], BLK)
+    periodic(96, sum(ends[:4], []), BLK + 1)
+    periodic(128, [e - CUT for e in ends[4][:BLK]] + [0, ends[5][0] - CUT], BLK + 1)
+    for n, v in (("round", ROUND), ("wipe", WIPE), ("nslope", -SLOPE), ("p8192", 8192.0), ("slope", SLOPE), ("nbig", -BIG / 64),
+                 ("nhalf", -0.5), ("magic", MAGIC), ("neg", -1.0)):
+        act(R(n), R("ident"), FN.Copy, scale=v)
+    ts(R("pow", 0, 128), R("ident"), 256.0, A.mult)
+    ts(R("qi"), R("qi"), 15, A.bitwise_and)
+    constants_sum = halving("pow") + [lambda: ts(R("nid"), R("ident"), -1.0, A.mult), lambda: cp(R("qf"), R("qi")),
+                                      lambda: cp(R("lrep"), R("qi"))]
+
+    def power(e):
+        return R("pow", 128 * (8 - e), 128 * (9 - e))
+
+    constants_key = halving("tri") + [
+        lambda: ts(R("bigc"), R("sel"), BIG, A.mult),
+        lambda: ts(R("kq"), col("qf", 0), 8192.0, A.mult, 2048 - HALF, A.add),
+        lambda: ts(R("unwipe", 0, 256), R("pow", 128 * (7 - 2 * SG[0]), 128 * (9 - 2 * SG[0])), -8 * MAGIC / 256, A.mult),
+        lambda: ts(R("unwipe", 256, 512), R("pow", 128 * (7 - 2 * SG[1]), 128 * (9 - 2 * SG[1])), -8 * MAGIC / 256, A.mult),
+        lambda: ts(R("none", 0, 16), R("jc", 0, 16), col("qf", 0), A.add, HALF + NW, A.add),
+        lambda: ts(R("none", 16, 32), R("jc", 0, 16), col("qf", 0), A.add, HALF + NW, A.add),
+        lambda: ts(R("kge"), R("kge"), 8192.0, A.mult, -HALF, A.add),
+        lambda: ts(R("bigu"), R("sel"), col("wts", 0), A.mult),
+        lambda: ts(R("bigv"), R("sel"), col("wts", 1), A.mult)]
+
+    whole = 16 * PERIOD
+    constants_write = [lambda n=n: ts(R("inval", 16 * n, 16 * n + 16), R("cnt", 0, 16), col("qf", 0), A.is_gt, 0.5, A.mult)
+                       for n, (c, o) in enumerate(PAIRS[:PERIOD]) if c == o] + [
+        lambda: ts(R("rti"), R("rti"), 15, A.bitwise_and),
+        lambda: cp(R("inval", whole, 2 * whole), R("inval", 0, whole)),
+        lambda: ts(R("cnt"), R("cnt"), 1.0, A.min),
+        lambda: ts(R("dg"), R("rti"), 0.0, A.is_equal),
+        lambda: cp(R("inval", 2 * whole, 4 * whole), R("inval", 0, 2 * whole)),
+        lambda: tt(R("rtf"), R("rti", 0, 128), R("blk"), A.add),
+        lambda: cp(R("inval", 4 * whole, WD), R("inval", 0, WD - 4 * whole)),
+        lambda: tt(R("row"), R("row"), R("dg"), A.mult),
+        lambda: op("V", V.tensor_tensor_scan, ["out"], out=R("dg"), data0=R("cnt"), data1=R("row"), initial=0.0, op0=A.mult,
+                   op1=A.add),
+        lambda: cp(R("lst", 0, 9), R("dg", 15, 144, 16))]
+    turns = [lambda d=d: ts(R("rot", 128 * d, 128 * d + 128), R("rtf"), float(d), A.is_equal) for d in range(16)]
+
+    def tolist(out, src, lo, hi, wt, first=True):
+        for q in range(16):
+            mm(out, R(wt, 16 - q, 144 - q), R(src, lo + q, hi, 16), first and q == 0, q == 15)
+
+    def before_sums():
+        mm(ps(4, 0, 256), R("sums", 0, 128), R("ones", 0, 256), True, False)
+
+    def sums():
+        for q in range(16):
+            mm(ps(4, q, 256, 16), R("mz", q, 2048, 16), R("uv"), False, False)
+        mm(ps(4, 0, 256), R("round"), R("ones", 0, 256), False, False)
+        mm(ps(4, 0, 256), R("sums", 128, 256), R("ones", 0, 256), False, False)
+        for q in range(16):
+            mm(ps(4, q, 256, 16), R("mz", q, 2048, 16), R("nuv"), False, q == 15)
+
+    def turn_keys():
+        mm(ps(5, 0, 128), R("p8192"), R("jc"), True, False)
+        mm(ps(5, 0, 128), R("h16"), R("nid"), False, True)
+
+    places = [lambda: act(R("hu"), ps(4, 0, 128), FN.Copy),
+              lambda: tt(ps(5, 0, 128), R("hu"), ps(4, 128, 256), A.mult),
+              lambda: act(R("hq"), R("hu"), FN.Identity, scale=-37.0 * 32, bias=NHALF),
+              lambda: tt(R("hs1"), R("hq"), ps(5, 0, 128), A.add),
+              lambda: ts(R("hh"), R("hs1"), 5, A.arith_shift_right, 4095, A.bitwise_and),
+              lambda: ts(R("h16"), R("hh"), -1.0, A.mult, 2048.0, A.add),
+              lambda: mm(ps(4, 0, 128), R("h16"), R("nid"), True, True),
+              turn_keys,
+              lambda: ts(R("hl"), ps(4, 0, 128), 2048.0, A.add),
+              lambda: act(R("base"), ps(5, 0, 128), FN.Identity, bias=R("kq"))]
+
+    def written():
+        return [lambda: cp(R("hi2"), ps(5, 0, 32)),
+                lambda: ts(R("hi2"), R("hi2"), 4095, A.bitwise_and),
+                lambda: tt(R("gp"), R("hi2", 0, 16), R("hi2", 16, 32), A.mult),
+                lambda: ts(R("gq"), R("hi2", 0, 16), 37.0 * 32, A.mult, -HALF, A.add),
+                lambda: tt(R("gp"), R("gp"), R("gq"), A.add),
+                lambda: ts(R("pl"), R("gp"), 5, A.arith_shift_right, 4095, A.bitwise_and)]
+
+    def before_probe(t, b):
+        if b in SG or b in SM:
+            mm(ps(b), R("wipe" if b in SG else "nslope"), bk(nbuf[t % 2], b), True, False)
+        mm(ps(b), R("nslope"), bk("mz", b), b not in SG and b not in SM, False)
+
+    def before_none(t):
+        mm(ps(7, 0, 256), power(-2), R("ones", 0, 256), True, False)
+        mm(ps(7, 0, 256), power(-1), R("zb%d" % t), False, False)
+
+    def before_firsts():
+        mm(ps(FB, 256, 512), R("magic"), R("c128"), True, False)
+
+    def before_count(h):
+        mm(ps(4 + h, 0, 64), R("nbig"), R("lim"), True, False)
+
+    def gather(t, b):
+        win = G(R("tab", 0, NW), R("hl", 32 * b, 32 * b + 32))
+        if b in SG:
+            act(bk("xy", b), win, FN.Copy)
+        else:
+            tt(bk("xy", b), win, bk(nbuf[t % 2], b), A.max)
+
+    def difference(t, b):
+        mm(ps(b), R("slope"), bk("xy", b), False, b not in SG)
+        if b in SG:
+            for h in range(2):
+                i = 2 * SG.index(b) + 1 - h
+                mm(ps(b, 256 * h, 256 * h + 256), R("unwipe", 128 * i, 128 * i + 128), mk("th", 2 * b + h), False, h == 1)
+
+    def failing(b):
+        if b in SG:
+            act(bk("ff", b), ps(b), FN.Abs, bias=NMAGIC)
+        else:
+            ts(bk("ff", b), ps(b), MAGIC, A.add, MAGIC, A.not_equal)
+
+    def firsts(b):
+        for k in (2 * b, 2 * b + 1):
+            mm(ps(FB, 256, 512), R("tri", 128 * k, 128 * k + 128), mk("ff", k), False, k == NK - 1)
+            if k < NK - 1:
+                mm(ps(FB, 256, 512), power(6 - k), R("nmag"), False, False)
+
+    def counts(h):
+        tolist(ps(4 + h, 0, 64), "ff", 1024 * h, 1024 * h + 1024, "bigc", first=False)
+
+    def thresholds(t):
+        return [lambda k=k: act(mk("th", k), mk(nbuf[t % 2], k), FN.Identity, scale=1.125 * 2 ** (8 - k) / OFF, bias=-2.0 ** (5 - k))
+                for k in range(NK)]
+
     ts(R("n0"), R("mini"), -OFF, A.mult, OFF, A.add)
+    for j in range(2):
+        ts(R("uv", 8 * j, 8 * j + 8), R("sel", 16, 144, 16), col("wts", j), A.mult)
+    for k in sorted(range(NK), key=lambda k: k // 2 not in SM):
+        if k // 2 in SM:
+            ts(mk("mz", k), R("zb0"), col("mini", k), A.mult)
+        else:
+            ts(mk("mz", k), R("zb0"), col("n0", k), A.max)
+    ts(R("nuv"), R("uv"), -1.0, A.mult)
+    before_sums()
+    sums()
     for k in range(NK):
-        ts(mk("mz", k), R("zb0"), col("n0", k), A.max)
-        if k == 3:
-            ts(R("bigu"), R("sel"), col("wts", 0), A.mult)
-            ts(R("bigv"), R("sel"), col("wts", 1), A.mult)
-    for k in range(NK):
-        act(mk("na", k), R("ones", 0, 256), FN.Identity, scale=col("n0", k))
-    sums(0)
-    sums(1)
-    constants_key()
+        if k // 2 in SG:
+            act(mk("na", k), R("ones", 0, 256), FN.Identity, scale=col("n0", k))
+    merge(constants_sum, [lambda k=k: ts(mk("na", k), R("ones", 0, 256), col("n0", k), A.mult) for k in range(NK) if k // 2 not in SG])
+    merge([thresholds(0)[k] for k in range(NK) if k // 2 in SG])
     mm(ps(6, 0, 256), R("ident"), R("zb0"), True, True)
     for b in range(4):
         before_probe(0, b)
     before_none(0)
-    chains, lists, more = constants_write()
-    merge(*chains)
-    merge(places(0), places(1), lists[:7])
-    merge(lists[7:])
-    thresholds(0, range(NK))
+    before_firsts()
+    merge(constants_key[0::2], places, constants_key[1::2])
     before_count(0)
     before_count(1)
 
+    late = [constants_write[:6], constants_write[6:10], [thresholds(0)[k] for k in range(NK) if k // 2 not in SG],
+            turns[:3], turns[3:6], constants_write[10:], turns[6:10], turns[10:13], turns[13:]]
+
     for t in range(STEPS):
         last = t == STEPS - 1
-        cur, nxt, z, zn, zs = nbuf[t % 2], nbuf[(t + 1) % 2], R("zb%d" % t), "zb%d" % (t + 1), "zs%d" % (t + 1)
+        cur, nxt, z, zn, nz = nbuf[t % 2], nbuf[(t + 1) % 2], R("zb%d" % t), "zb%d" % (t + 1), R("nz%d" % t)
 
         def moved(lo, hi):
             return G(R(cur), R("mvu", 16 * lo - 16, 16 * hi - 16))
 
-        for b in range(4):
-            gather(t, b)
-        difference(t, 0)
-        difference(t, 1)
-        mm(ps(7, 0, 256), R("nhalf"), mk("xy", 0), False, False)
-        mm(ps(7, 0, 256), R("magic"), R("ones", 0, 256), False, True)
-        failing(0)
-        difference(t, 2)
-        difference(t, 3)
-        failing(1)
-        act(R("tab", NW, NW + NP), ps(7, 0, 256), FN.Identity, bias=NMAGIC)
-        failing(2)
-        tt(R("base"), R("hh"), R("kc"), A.add)
-        prefix(0)
-        counts(0)
-        failing(3)
-        prefix(1)
-        firsts(0)
-        prefix(2)
-        counts(1)
-        prefix(3)
-        firsts(1)
-        keys(0, R("ka"))
-        tt(R("kb"), R("ka"), R("none"), A.min)
-        firsts(2)
-        firsts(3)
-        keys(1, R("kc2"))
-        for b in range(4):
-            weigh(b)
-        tt(R("kd"), R("kc2"), R("kb"), A.min)
-        tt(R("key"), R("kd", 0, 16), R("kd", 16, 32), A.min)
-        act(R("ssb"), ps(4, 0, 256), FN.Copy)
-        ts(R("hs"), R("key"), 8191, A.bitwise_and)
-        ts(R("ju"), R("key"), 1.0 / 8192, A.mult, 1024.0, A.add)
-        cp(R("hsu"), R("hs"))
-        if not last:
-            ts(R("nm"), R("key"), HALF, A.is_ge)
-        tt(R("dz%d" % t), G(R("tab"), R("hsu")), z, A.subtract)
-        if not last:
-            rid, pid = topo.addr(nxt_core, core)
-            hold("G", [R("dz%d" % t)], [])
-            g.remote_dma(out_ap=ap(R(zs)), in_ap=ap(R("dz%d" % t)), remote_sem=T.sem["arr%d" % (t + 1)], local_sem=T.sem["sent"],
-                         pid=pid, routing_id=rid, dma_engine_mask=topo.mask(core, nxt_core))
-            note("arr%d" % (t + 1), len(topo.engines(prv_core, core)), [], [R(zs)])
-        tt(R("ub"), G(R("th"), R("ju")), R("ssb"), A.is_le)
-        tt(R("ge"), G(R("key"), R("lrep", 0, 7)), R("kge"), A.is_ge)
-        if last:
-            tt(R("mv"), R("mvb"), R("ge"), A.subtract)
-            ts(R("mvu"), R("mv"), 256.0, A.mult)
-            store(T["ym"][:, 0:256], R("ub"))
-            for lo, hi in ((1, 3), (3, 5), (5, 7), (7, 8)):
-                src = G(R(cur), R("mvu", 16 * lo - 16, 16 * hi - 16))
-                if lo in (1, 5):
-                    act(R("mo", 256 * lo, 256 * hi), src, FN.Relu, scale=-1.0, bias=ONE)
-                else:
-                    ts(R("mo", 256 * lo, 256 * hi), src, 1.0, A.is_lt)
-                store(T["ym"][:, 256 * lo:256 * hi], R("mo", 256 * lo, 256 * hi))
-            act(R("nz%d" % t), R("dz%d" % t), FN.Abs)
-            store(T["yz"][:, NP * t:NP * t + NP], R("nz%d" % t))
-            break
-        tt(R("uz"), R("ub"), ps(6, 0, 256), A.mult)
-        tt(R("mv"), R("mvb"), R("ge"), A.subtract)
-        ts(R("mvu"), R("mv"), 256.0, A.mult)
-        tolist(ps(5, 0, 16), "uz", 0, 256, "bigu")
-        tolist(ps(5, 16, 32), "uz", 0, 256, "bigv")
-        mm(ps(4, 0, 16), R("ones", 0, 128), R("nm"), True, True)
-        act(mk(nxt, 0), R("ub"), FN.Identity, scale=-OFF, bias=POFF)
-        cp(bk(nxt, 1), moved(2, 4))
-        for lo, hi in ((1, 2), (4, 6), (6, 8)):
-            act(R(nxt, 256 * lo, 256 * hi), moved(lo, hi), FN.Copy)
-        act(R("par"), ps(4, 0, 16), FN.Identity, scale=0.5, bias=M64, accum_out=col("px", 0))
-        parity = [lambda: act(col("px", 1), col("px", 0), FN.Identity, bias=PMAGIC),
-                  lambda: act(col("px", 2), col("px", 1), FN.Identity, bias=NMAGIC),
-                  lambda: act(col("px", 3), col("px", 2), FN.Identity, scale=-1.0, bias=col("px", 0)),
-                  lambda: act(R("lim"), R("two"), FN.Identity, scale=col("px", 3), bias=P175)]
-        mm(ps(7, 0, WD), R("ident"), R("inval"), True, False)
-        for b in SG:
-            mm(ps(b), R("neg"), bk(nxt, b), True, False)
-        merge(hashing(ps(5, 0, 32), "hi2", R("gp"), R("gq"), R("pl"), 16), *[more[i::4] for i in range(4)])
-        more = []
-        ts(R("hx"), G(R("pl"), R("lpair")), -2048.0, A.add)
-        cp(G(R("clamp"), col("lslot", 0)), R("pl"))
-        for d in range(16):
-            mm(ps(7, d, WD, 16), R("rot", 128 * d, 128 * d + 128), R("hx", 0, NPAIR), False, False)
-        act(R(zn), R(zs), FN.Abs)
-        act(ps(6, 0, 256), R(zs), FN.Abs)
-        for b in SG:
+        def none():
+            mm(ps(7, 0, 256), R("nhalf"), mk("xy", 0), False, False)
+            mm(ps(7, 0, 256), R("magic"), R("ones", 0, 256), False, True)
+
+        def send():
+            act(nz, R("dz"), FN.Abs)
+            if not last:
+                rid, pid = topo.addr(nxt_core, core)
+                hold("G", [nz], [])
+                g.remote_dma(out_ap=ap(R(zn)), in_ap=ap(nz), remote_sem=T.sem["arr%d" % (t + 1)], local_sem=T.sem["sent"],
+                             pid=pid, routing_id=rid, dma_engine_mask=topo.mask(core, nxt_core))
+                note("arr%d" % (t + 1), len(topo.engines(prv_core, core)), [], [R(zn)])
+            store(T["yz"][:, NP * t:NP * t + NP], nz)
+
+        def move(i):
+            lo, hi = MOVES[i]
+            if i in VMOVE:
+                cp(R(nxt, 256 * lo, 256 * hi), moved(lo, hi))
+            else:
+                act(R(nxt, 256 * lo, 256 * hi), moved(lo, hi), FN.Copy)
+
+        def others():
+            for d in range(16):
+                mm(ps(7, d, WD, 16), R("rot", 128 * d, 128 * d + 128), R("hx", 0, NPAIR), False, False)
+
+        def own():
+            for d in range(16):
+                mm(ps(7, d, WD, 16), R("nid"), R("hx", 32, 32 + NPAIR), False, d == 15)
+
+        def header(b):
             for h in range(2):
                 mm(ps(b, 256 * h, 256 * h + 256), R("ident"), R(zn), False, h == 1)
-        for d in range(16):
-            mm(ps(7, d, WD, 16), R("nid"), R("hx", 32, 32 + NPAIR), False, d == 15)
-        for b in SG:
-            act(bk("mz", b), ps(b), FN.Relu)
-        for k in range(NK):
-            if k // 2 not in SG:
-                tt(mk("mz", k), mk(nxt, k), ps(6, 0, 256), A.max)
-        ts(R("eq"), ps(7, 0, WD), 0.0, A.is_equal, 8192.0, A.mult)
-        sums(0)
-        sums(1)
-        op("V", V.tensor_tensor_scan, ["out"], out=R("st"), data0=R("eq"), data1=R("clamp", 0, WD), initial=0.0, op0=A.add,
-           op1=A.min)
-        merge(parity, [lambda k=k: thresholds(t + 1, [k]) for k in range(NK)])
-        act(R("nz%d" % t), R("dz%d" % t), FN.Abs)
-        store(T["yz"][:, NP * t:NP * t + NP], R("nz%d" % t))
-        for b in range(4):
-            before_probe(t + 1, b)
-        before_none(t + 1)
-        scatters = [lambda m=m, blk=blk: cp(G(R("tab"), R("scu", 4 * m, 4 * m + len(blk))),
-                                            R("zb%d" % t, 16 * blk[0], 16 * blk[-1] + 16)) for m, blk in enumerate(BLOCKS)][::-1]
-        h0, h1 = places(0), places(1)
-        cp(R("scu"), G(R("st"), R("lend")))
-        merge(h0[:3], scatters[:3])
-        merge(h1[:3], h0[3:6], scatters[3:])
-        merge(h1[3:], h0[6:])
-        before_count(0)
-        before_count(1)
+
+        def part(name, h):
+            return R(name, CUT, WD) if h else R(name, 0, CUT)
+
+        def scan(h):
+            op("V", V.tensor_tensor_scan, ["out"], out=part("st", h), data0=part("eq", h), data1=part("clamp", h), initial=0.0,
+               op0=A.min, op1=A.max)
+
+        def scatter(m):
+            blk = BLOCKS[m]
+            cp(G(R("tab"), R("scu", 4 * m, 4 * m + len(blk))), R("zb%d" % t, 16 * blk[0], 16 * blk[-1] + 16))
+
+        def result(i):
+            lo, hi = ((1, 3), (3, 5), (5, 7), (7, 8))[i]
+            if i % 2 == 0:
+                act(R("mo", 256 * lo, 256 * hi), moved(lo, hi), FN.Relu, scale=-1.0, bias=ONE)
+            else:
+                ts(R("mo", 256 * lo, 256 * hi), moved(lo, hi), 1.0, A.is_lt)
+            store(T["ym"][:, 256 * lo:256 * hi], R("mo", 256 * lo, 256 * hi))
+
+        parity = [lambda: act(R("par"), ps(4, 0, 16), FN.Identity, scale=0.5, bias=M64, accum_out=col("px", 0)),
+                  lambda: act(col("px", 1), col("px", 0), FN.Identity, bias=PMAGIC),
+                  lambda: act(col("px", 2), col("px", 1), FN.Identity, bias=NMAGIC),
+                  lambda: act(col("px", 3), col("px", 2), FN.Identity, scale=-1.0, bias=col("px", 0)),
+                  lambda: act(R("lim"), R("c128", 0, 64), FN.Identity, scale=col("px", 3), bias=112.0)]
+        numbered = {
+            "g": lambda b: gather(t, b), "d": lambda b: difference(t, b), "f": failing, "r": firsts, "c": counts,
+            "y": lambda h: tt(R("ky", 64 * h, 64 * h + 64), R("base", 64 * h, 64 * h + 64), ps(4 + h, 0, 64), A.max),
+            "k": lambda h: tt(R("kc" if h else "ka"), R("ky", 64 * h, 64 * h + 32), R("ky", 64 * h + 32, 64 * h + 64), A.min),
+            "m": move, "p": lambda i: parity[i](), "w": lambda i: written()[i](), "z": header,
+            "n": lambda b: mm(ps(b), R("neg"), bk(nxt, b), True, False),
+            "x": lambda b: act(bk("mz", b), ps(b), FN.Relu),
+            "v": lambda k: tt(mk("mz", k), mk(nxt, k), ps(6, 0, 256), A.max),
+            "e": lambda h: act(part("eq", h), part("ps7", h), FN.Abs, scale=4 * TOP), "a": scan,
+            "u": lambda h: ts(R("scu", 16 * h, 16 * h + 16), G(part("st", h), col("lst", 6 + 2 * h)), -1.0, A.mult, TOP, A.add),
+            "s": scatter, "h": lambda i: places[i](), "t": lambda k: thresholds(t + 1)[k](),
+            "b": lambda b: before_probe(t + 1, b), "l": before_count, "o": result,
+            "q": lambda i: merge(late[i] if t == 0 else [])}
+        named = {
+            "none": none, "ncol": lambda: act(R("tab", NW, NW + NP), ps(7, 0, 256), FN.Identity, bias=NMAGIC),
+            "kb": lambda: tt(R("kb"), R("ka"), R("none"), A.min),
+            "kd": lambda: tt(R("kd"), R("kc"), R("kb"), A.min),
+            "key": lambda: tt(R("key"), R("kd", 0, 16), R("kd", 16, 32), A.min),
+            "ssb": lambda: act(R("ssb"), ps(FB, 256, 512), FN.Identity, scale=-1.0, bias=PMAGIC),
+            "hs": lambda: ts(R("hs"), R("key"), 8191, A.bitwise_and),
+            "ju": lambda: ts(R("ju"), R("key"), 1.0 / 8192, A.mult, 1024.0, A.add),
+            "hsu": lambda: cp(R("hsu"), R("hs")),
+            "ge": lambda: tt(R("ge"), G(R("key"), R("lrep")), R("kge"), A.is_lt),
+            "dz": lambda: tt(R("dz"), G(R("tab"), R("hsu")), z, A.subtract), "send": send,
+            "stay": lambda: mm(ps(7, 0, 112), R("ident"), R("jc", 0, 112), True, False),
+            "down": lambda: mm(ps(7, 0, 112), power(8), R("ge", 0, 112), False, True),
+            "mvu": lambda: ts(R("mvu"), ps(7, 0, 112), col("qf", 0), A.add),
+            "ub": lambda: tt(R("ub"), G(R("th"), R("ju")), R("ssb"), A.is_le),
+            "uz": lambda: tt(R("uz"), R("ub"), ps(6, 0, 256), A.mult),
+            "su": lambda: tolist(ps(5, 0, 16), "uz", 0, 256, "bigu"), "sv": lambda: tolist(ps(5, 16, 32), "uz", 0, 256, "bigv"),
+            "nm": lambda: mm(ps(4, 0, 16), R("ones", 0, 128), R("ge", 112, 128), True, True),
+            "code": lambda: act(mk(nxt, 0), R("ub"), FN.Identity, scale=-OFF, bias=POFF),
+            "inval": lambda: mm(ps(7, 0, WD), R("ident"), R("inval"), True, False),
+            "hx": lambda: ts(R("hx"), G(R("pl"), R("lst", 0, 4)), -2048.0, A.add),
+            "npl": lambda: ts(R("npl"), R("pl"), -1.0, A.mult, TOP, A.add),
+            "slot": lambda: cp(G(R("clamp"), col("lst", 4)), R("npl")),
+            "others": others, "own": own, "zps": lambda: mm(ps(6, 0, 256), R("ident"), R(zn), True, True),
+            "presum": before_sums, "sums": sums, "prenone": lambda: before_none(t + 1), "prefirst": before_firsts,
+            "out": lambda: store(T["ym"][:, 0:256], R("ub"))}
+        for name in (PROBE + " " + (LAST if last else WRITE)).split():
+            if name in named:
+                named[name]()
+            else:
+                numbered[name[0]](int(name[1]))
     g.sync.wait_ge(T.sem["outs"], stored[0])
     for e in QUEUES:
         g.sync.wait_ge(T.sem[semof[e]], count[e])

import numpy as np
from concourse.mybir import dt, AluOpType, AxisListType, ActivationFunctionType

A = AluOpType
FN = ActivationFunctionType
STEPS, NP, NK, NW = 6, 256, 8, 4096
MAGIC = 12582912.0
ROUND = MAGIC * 4096
CENTRE = 4096.0 * 2040
SLOPE = 185.0 / 32768
OFF = 4096.0
WIPE = 9 * MAGIC / OFF
BIG = 2.0 ** 25
HALF = 2.0 ** 23
TOP = 8192.0
B16, F32, I32, U16, F16 = "bfloat16", "float32", "int32", "uint16", "float16"
SG = (0, 2)
SM = (0, 2)
MOVES = ((1, 2), (2, 4), (4, 6), (6, 8))
VMOVE = (1,)
FB = 6
PROBE = "g1 d1 g0 g3 d0 d3 g2 f0 d2 f2 f1 q0 c0 none ncol f3 q1 q2 y0 k0 kb c1 y1 k1 kd key r0 hs r1 ju hsu r2 r3 ssb stay"
WRITE = "ge down dz mvu q3 ub q4 uz nm send m0 su sv inval m1 q5 w0 q6 w1 q7 w3 code m2 n2 m3 t4 w2 q8 w4 n0 t7 zps z2 p0 x2 w5 z0 x0 hx others v7 p1 v6 own e1 e0 v2 npl presum v3 sums b3 slot p2 a1 u1 b1 a0 h0 h2 s5 t1 p3 t2 t3 u0 t5 s4 h1 prenone s3 b0 h3 h4 s2 p4 h5 h6 s1 h7 t6 h9 h8 l0 t0 l1 prefirst b2 s0"
LAST = "ge dz down send mvu ub out o0 o1 o2 o3"
BLK = 3
BLOCKS = [list(range(c, min(c + BLK, 16))) for c in range(0, 16, BLK)]
PAIRS = [(c, o) for blk in BLOCKS for c in blk for o in range(c, blk[0] - 1, -1)]
NPAIR = len(PAIRS)
WD = 16 * NPAIR
PERIOD = BLK * (BLK + 1) // 2
CUT = 16 * PERIOD * 4

_SB = {
    "tab": (NW + NP, B16), "na": (2048, B16), "nb": (2048, B16), "th": (2064, B16), "mz": (2048, B16), "xy": (2048, B16),
    "ff": (2048, B16), "tri": (1024, B16), "nmag": (256, B16), "c128": (256, B16), "mini": (8, B16), "wts": (2, B16),
    "ones": (256, B16), "n0": (8, F32), "ident": (128, B16), "slope": (128, B16), "nslope": (128, B16), "wipe": (128, B16),
    "unwipe": (512, B16), "nhalf": (128, B16), "magic": (128, B16), "nbig": (128, B16), "pow": (11 * 128, B16),
    "neg": (128, B16), "round": (128, B16), "p8192": (128, B16), "sums": (256, B16),
    "sel": (144, B16), "bigu": (144, B16), "bigv": (144, B16), "bigc": (144, B16), "blk": (128, B16), "uv": (16, B16),
    "nuv": (16, B16), "rot": (2048, F16), "nid": (128, F16), "rti": (144, I32), "rtf": (128, B16), "inval": (WD, B16),
    "clamp": (16 * PERIOD * len(BLOCKS), F32), "qi": (8, I32), "qf": (8, F32), "jc": (128, B16), "kq": (1, F32),
    "kge": (128, F32), "none": (32, F32), "row": (144, F32), "lrep": (8, U16), "lst": (10, U16),
    "hu": (128, F32), "hq": (128, F32), "hs1": (128, I32), "hh": (128, I32), "h16": (128, F16), "hl": (128, U16),
    "hi2": (32, I32), "gp": (16, I32), "gq": (16, I32), "pl": (16, I32), "npl": (16, F32), "base": (128, F32), "ky": (128, F32),
    "ka": (32, F32), "kb": (32, F32), "kc": (32, F32), "kd": (32, F32), "key": (16, I32), "hs": (16, I32), "hsu": (16, U16),
    "ju": (16, U16), "ge": (128, B16), "mvu": (112, U16), "ssb": (256, B16), "ub": (256, B16), "uz": (256, B16), "dz": (256, B16),
    "hx": (64, F16), "eq": (WD, B16), "st": (WD, F32), "scu": (32, U16), "par": (16, F32), "px": (8, F32), "lim": (64, B16),
    "mo": (2048, B16), "cnt": (144, F32), "dg": (144, F32),
}
SCRATCH = {}
for _n in _SB:
    SCRATCH[_n] = ("sbuf", [128, _SB[_n][0]], _SB[_n][1])
for _t in range(STEPS):
    SCRATCH["zb%d" % _t] = ("sbuf", [128, NP], B16)
    SCRATCH["nz%d" % _t] = ("sbuf", [128, NP], B16)
for _b in range(8):
    SCRATCH["ps%d" % _b] = ("psum", [128, 512], F32)

SEMAPHORES = ["sv", "ss", "sp", "sg", "sent", "ldw", "ldm", "ldz", "ldx", "outs"] + ["arr%d" % t for t in range(1, STEPS)]
QUEUES = ("V", "S", "P", "G")


def rank_program(g, core, T, topo):
    rank = T.rank_of(core)
    if rank is None:
        return
    nxt_core = T.cores[(rank + 1) % len(T.cores)]
    prv_core = T.cores[(rank - 1) % len(T.cores)]
    V, S, P = g.vector, g.scalar, g.tensor

    def R(name, lo=0, hi=None, step=1):
        return (name, lo, SCRATCH[name][1][1] if hi is None else hi, step)

    def G(win, off):
        return win + (off,)

    def ap(r):
        a = T[r[0]][:, r[1]:r[2]:r[3]] if r[3] != 1 else T[r[0]][:, r[1]:r[2]]
        return a.indirect(ap(r[4])) if len(r) > 4 else a

    semof = {"V": "sv", "S": "ss", "P": "sp", "G": "sg"}
    waiter = {"V": V.wait_ge, "S": S.wait_ge, "P": P.wait_ge, "G": g.wait_ge, "Y": g.sync.wait_ge}
    count = {"V": 0, "S": 0, "P": 0, "G": 0}
    known = {"V": {}, "S": {}, "P": {}, "G": {}, "Y": {}}
    snap, wrote, read, bank = {}, {}, {}, {}

    def marks(book, r):
        return [(f, int(a[r[1]:r[2]].max())) for f, a in book.get(r[0], {}).items()]

    def hold(e, rd, wr):
        deps = {}
        found = []
        for r in rd:
            found += marks(wrote, r)
        for r in wr:
            found += marks(wrote, r) + marks(read, r)
        for r in rd + wr:
            found += [x for x in bank.get(r[0], {}).items() if x[0] != e]
        for f, n in found:
            if not (e == "P" and f == "P") and known[e].get(f, 0) < n and deps.get(f, 0) < n:
                deps[f] = n
        for f in sorted(deps):
            if not any(f2 != f and snap.get((f2, n2), {}).get(f, 0) >= deps[f] for f2, n2 in deps.items()):
                waiter[e](T.sem[semof.get(f, f)], deps[f])
        for f, n in deps.items():
            for f2, n2 in snap.get((f, n), {}).items():
                known[e][f2] = max(known[e].get(f2, 0), n2)
            known[e][f] = max(known[e].get(f, 0), n)

    def note(f, n, rd, wr):
        for book, rs in ((read, rd), (wrote, wr)):
            for r in rs:
                if SCRATCH[r[0]][0] == "psum":
                    bank.setdefault(r[0], {})[f] = n
                marks_of = book.setdefault(r[0], {})
                if f not in marks_of:
                    marks_of[f] = np.zeros(SCRATCH[r[0]][1][1], np.int64)
                marks_of[f][r[1]:r[2]] = n

    def op(e, call, outs, row=None, **kw):
        wr = [kw[k] for k in outs]
        rd = [v for k, v in kw.items() if isinstance(v, tuple) and k not in outs]
        rd += [r[4] for r in rd + wr if len(r) > 4]
        hold(e, rd, wr)
        count[e] += 1
        args = {k: ap(v) if isinstance(v, tuple) else v for k, v in kw.items()}
        if row is not None:
            args[outs[0]] = T[wr[0][0]][row:row + 1, wr[0][1]:wr[0][2]]
        call(**args).then_inc(T.sem[semof[e]], 1)
        snap[(e, count[e])] = dict(known[e])
        note(e, count[e], rd, wr)

    def load(q, sem, r, src):
        q.dma_start(out=ap(r), in_=src).then_inc(T.sem[sem], 16)
        note(sem, 16, [], [r])

    stored = [0]

    def store(dst, r):
        hold("Y", [r], [])
        g.sync.dma_start(out=dst, in_=ap(r)).then_inc(T.sem["outs"], 16)
        stored[0] += 16

    def tt(out, in0, in1, o):
        op("V", V.tensor_tensor, ["out"], out=out, in0=in0, in1=in1, op=o)

    def ts(out, in0, s1, o1, s2=None, o2=None):
        more = {} if o2 is None else {"op1": o2}
        op("V", V.tensor_scalar, ["out"], out=out, in0=in0, scalar1=s1, scalar2=s2, op0=o1, **more)

    def cp(out, in_):
        op("V", V.tensor_copy, ["out"], out=out, in_=in_)

    def act(out, in_, func, **kw):
        op("S", S.activation, ["out"] + [k for k in kw if k == "accum_out"], out=out, in_=in_, func=func, **kw)

    def mm(out, lhsT, rhs, start, stop):
        op("P", P.matmul, ["out"], out=out, lhsT=lhsT, rhs=rhs, start=start, stop=stop)

    def fill(r, val, row=None):
        op("V", V.memset, ["ap"], row, ap=r, constant=val)

    def select(r, pattern, cmp, val, base, mul):
        op("G", g.affine_select, ["out"], out=r, in_=r, pattern=pattern, compare_op=cmp, fill=val, base=base,
           channel_multiplier=mul)

    def iota(r, pattern, base, mul):
        kw = {} if SCRATCH[r[0]][2] == I32 else {"allow_small_or_imprecise_dtypes": True}
        op("G", g.iota, ["out"], out=r, pattern=pattern, base=base, channel_multiplier=mul, **kw)

    def ps(b, lo=0, hi=512, step=1):
        return ("ps%d" % b, lo, hi, step)

    def bk(name, b):
        return R(name, 512 * b, 512 * b + 512)

    def mk(name, k):
        return R(name, 256 * k, 256 * k + 256)

    def col(name, j):
        return R(name, j, j + 1)

    def merge(*chains):
        for i in range(max(len(c) for c in chains)):
            for c in chains:
                if i < len(c):
                    c[i]()

    nbuf = ["na", "nb"]
    NMAGIC, POFF, ONE, M64, PMAGIC, NHALF = -MAGIC, OFF, 1.0, -1.0 / 64, MAGIC, -HALF

    load(g.sync, "ldz", R("zb0"), T["z0"][:])
    load(g.scalar, "ldm", R("mini"), T["m0"][:])
    load(g.sync, "ldw", R("wts"), T["wt"][:])
    load(g.scalar, "ldx", R("tab", 0, NW), T["xr"][:])

    def halving(name):
        n, calls = 128, []
        while n < SCRATCH[name][1][1]:
            m = min(n, SCRATCH[name][1][1] - n)
            calls.append(lambda n=n, m=m: ts(R(name, n, n + m), R(name, 0, m), 2.0 ** -(n // 128), A.mult))
            n += m
        return calls

    def periodic(lo, values, period):
        for i in range(min(period, len(values))):
            v = values[i::period]
            iota(R("row", lo + i, lo + i + period * (len(v) - 1) + 1, period), [[v[1] - v[0] if len(v) > 1 else 0, len(v)]], v[0], 0)

    fill(R("ident"), 1.0)
    fill(R("sel"), 1.0)
    select(R("ident"), [[1, 128]], A.is_equal, 0.0, 0, -1)
    fill(R("sums"), 0.0)
    fill(R("tri", 0, 128), 128.0 / 32)
    fill(R("blk"), 0.0)
    merge([lambda row=row, v=v: fill(R("sums", 0, 128), v, row) for row, v in ((0, -HALF), (32, HALF - CENTRE - 2048), (64, 0.5))],
          [lambda row=row, v=v: fill(R("sums", 128, 256), v, row) for row, v in ((0, -ROUND), (32, CENTRE))],
          [lambda n=n, v=v: fill(R(n), v) for n, v in (("ones", 1.0), ("row", 0.0), ("inval", 0.0), ("nmag", -MAGIC),
                                                       ("c128", 128.0), ("lim", 80.0))])
    fill(R("th", 2048, 2064), 1.0)
    select(R("sel"), [[-16, 9], [-1000, 16]], A.is_ge, 0.0, 16, 1)
    iota(R("qi"), [[0, 8]], 0, 1)
    select(R("sel"), [[16, 9], [-1000, 16]], A.is_ge, 0.0, -1, -1)
    iota(R("jc"), [[256, 8], [16, 16]], 0, 0)
    select(R("tri", 0, 128), [[-16, 8], [0, 16]], A.is_ge, 0.0, 0, 1)
    iota(R("kge"), [[256, 8], [0, 16]], 256, 0)
    select(R("tri", 0, 128), [[1, 128]], A.is_ge, 0.0, -1, -1)
    iota(R("cnt"), [[0, 9], [1, 16]], 0, 0)
    select(R("tri", 0, 128), [[1, 128]], A.not_equal, -128.0 * 33 / 64, 0, -1)
    iota(R("rti"), [[1, 144]], 128, -1)
    select(R("blk"), [[-16, 8], [0, 16]], A.is_ge, 100.0, 0, 1)
    iota(R("clamp"), [[0, len(BLOCKS)], [16, PERIOD], [0, 16]], int(TOP) - NW - 16 * (PERIOD - 1), -1)
    select(R("blk"), [[16, 8], [0, 16]], A.is_ge, 100.0, 15, -1)
    ends = [[16 * PAIRS.index((c, blk[0])) + 15 for c in blk] + [0] * (BLK + 1 - len(blk)) for blk in BLOCKS]
    periodic(0, [o for c, o in PAIRS], PERIOD)
    periodic(32, [c for c, o in PAIRS], PERIOD)
    periodic(64, [16 * PAIRS.index((c, c)) for c in range(16)], BLK)
    periodic(96, sum(ends[:4], []), BLK + 1)
    periodic(128, [e - CUT for e in ends[4][:BLK]] + [0, ends[5][0] - CUT], BLK + 1)
    for n, v in (("round", ROUND), ("wipe", WIPE), ("nslope", -SLOPE), ("p8192", 8192.0), ("slope", SLOPE), ("nbig", -BIG / 64),
                 ("nhalf", -0.5), ("magic", MAGIC), ("neg", -1.0)):
        act(R(n), R("ident"), FN.Copy, scale=v)
    ts(R("pow", 0, 128), R("ident"), 256.0, A.mult)
    ts(R("qi"), R("qi"), 15, A.bitwise_and)
    constants_sum = halving("pow") + [lambda: ts(R("nid"), R("ident"), -1.0, A.mult), lambda: cp(R("qf"), R("qi")),
                                      lambda: cp(R("lrep"), R("qi"))]

    def power(e):
        return R("pow", 128 * (8 - e), 128 * (9 - e))

    constants_key = halving("tri") + [
        lambda: ts(R("bigc"), R("sel"), BIG, A.mult),
        lambda: ts(R("kq"), col("qf", 0), 8192.0, A.mult, 2048 - HALF, A.add),
        lambda: ts(R("unwipe", 0, 256), R("pow", 128 * (7 - 2 * SG[0]), 128 * (9 - 2 * SG[0])), -8 * MAGIC / 256, A.mult),
        lambda: ts(R("unwipe", 256, 512), R("pow", 128 * (7 - 2 * SG[1]), 128 * (9 - 2 * SG[1])), -8 * MAGIC / 256, A.mult),
        lambda: ts(R("none", 0, 16), R("jc", 0, 16), col("qf", 0), A.add, HALF + NW, A.add),
        lambda: ts(R("none", 16, 32), R("jc", 0, 16), col("qf", 0), A.add, HALF + NW, A.add),
        lambda: ts(R("kge"), R("kge"), 8192.0, A.mult, -HALF, A.add),
        lambda: ts(R("bigu"), R("sel"), col("wts", 0), A.mult),
        lambda: ts(R("bigv"), R("sel"), col("wts", 1), A.mult)]

    whole = 16 * PERIOD
    constants_write = [lambda n=n: ts(R("inval", 16 * n, 16 * n + 16), R("cnt", 0, 16), col("qf", 0), A.is_gt, 0.5, A.mult)
                       for n, (c, o) in enumerate(PAIRS[:PERIOD]) if c == o] + [
        lambda: ts(R("rti"), R("rti"), 15, A.bitwise_and),
        lambda: cp(R("inval", whole, 2 * whole), R("inval", 0, whole)),
        lambda: ts(R("cnt"), R("cnt"), 1.0, A.min),
        lambda: ts(R("dg"), R("rti"), 0.0, A.is_equal),
        lambda: cp(R("inval", 2 * whole, 4 * whole), R("inval", 0, 2 * whole)),
        lambda: tt(R("rtf"), R("rti", 0, 128), R("blk"), A.add),
        lambda: cp(R("inval", 4 * whole, WD), R("inval", 0, WD - 4 * whole)),
        lambda: tt(R("row"), R("row"), R("dg"), A.mult),
        lambda: op("V", V.tensor_tensor_scan, ["out"], out=R("dg"), data0=R("cnt"), data1=R("row"), initial=0.0, op0=A.mult,
                   op1=A.add),
        lambda: cp(R("lst", 0, 9), R("dg", 15, 144, 16))]
    turns = [lambda d=d: ts(R("rot", 128 * d, 128 * d + 128), R("rtf"), float(d), A.is_equal) for d in range(16)]

    def tolist(out, src, lo, hi, wt, first=True):
        for q in range(16):
            mm(out, R(wt, 16 - q, 144 - q), R(src, lo + q, hi, 16), first and q == 0, q == 15)

    def before_sums():
        mm(ps(4, 0, 256), R("sums", 0, 128), R("ones", 0, 256), True, False)

    def sums():
        for q in range(16):
            mm(ps(4, q, 256, 16), R("mz", q, 2048, 16), R("uv"), False, False)
        mm(ps(4, 0, 256), R("round"), R("ones", 0, 256), False, False)
        mm(ps(4, 0, 256), R("sums", 128, 256), R("ones", 0, 256), False, False)
        for q in range(16):
            mm(ps(4, q, 256, 16), R("mz", q, 2048, 16), R("nuv"), False, q == 15)

    def turn_keys():
        mm(ps(5, 0, 128), R("p8192"), R("jc"), True, False)
        mm(ps(5, 0, 128), R("h16"), R("nid"), False, True)

    places = [lambda: act(R("hu"), ps(4, 0, 128), FN.Copy),
              lambda: tt(ps(5, 0, 128), R("hu"), ps(4, 128, 256), A.mult),
              lambda: act(R("hq"), R("hu"), FN.Identity, scale=-37.0 * 32, bias=NHALF),
              lambda: tt(R("hs1"), R("hq"), ps(5, 0, 128), A.add),
              lambda: ts(R("hh"), R("hs1"), 5, A.arith_shift_right, 4095, A.bitwise_and),
              lambda: ts(R("h16"), R("hh"), -1.0, A.mult, 2048.0, A.add),
              lambda: mm(ps(4, 0, 128), R("h16"), R("nid"), True, True),
              turn_keys,
              lambda: ts(R("hl"), ps(4, 0, 128), 2048.0, A.add),
              lambda: act(R("base"), ps(5, 0, 128), FN.Identity, bias=R("kq"))]

    def written():
        return [lambda: cp(R("hi2"), ps(5, 0, 32)),
                lambda: ts(R("hi2"), R("hi2"), 4095, A.bitwise_and),
                lambda: tt(R("gp"), R("hi2", 0, 16), R("hi2", 16, 32), A.mult),
                lambda: ts(R("gq"), R("hi2", 0, 16), 37.0 * 32, A.mult, -HALF, A.add),
                lambda: tt(R("gp"), R("gp"), R("gq"), A.add),
                lambda: ts(R("pl"), R("gp"), 5, A.arith_shift_right, 4095, A.bitwise_and)]

    def before_probe(t, b):
        if b in SG or b in SM:
            mm(ps(b), R("wipe" if b in SG else "nslope"), bk(nbuf[t % 2], b), True, False)
        mm(ps(b), R("nslope"), bk("mz", b), b not in SG and b not in SM, False)

    def before_none(t):
        mm(ps(7, 0, 256), power(-2), R("ones", 0, 256), True, False)
        mm(ps(7, 0, 256), power(-1), R("zb%d" % t), False, False)

    def before_firsts():
        mm(ps(FB, 256, 512), R("magic"), R("c128"), True, False)

    def before_count(h):
        mm(ps(4 + h, 0, 64), R("nbig"), R("lim"), True, False)

    def gather(t, b):
        win = G(R("tab", 0, NW), R("hl", 32 * b, 32 * b + 32))
        if b in SG:
            act(bk("xy", b), win, FN.Copy)
        else:
            tt(bk("xy", b), win, bk(nbuf[t % 2], b), A.max)

    def difference(t, b):
        mm(ps(b), R("slope"), bk("xy", b), False, b not in SG)
        if b in SG:
            for h in range(2):
                i = 2 * SG.index(b) + 1 - h
                mm(ps(b, 256 * h, 256 * h + 256), R("unwipe", 128 * i, 128 * i + 128), mk("th", 2 * b + h), False, h == 1)

    def failing(b):
        if b in SG:
            act(bk("ff", b), ps(b), FN.Abs, bias=NMAGIC)
        else:
            ts(bk("ff", b), ps(b), MAGIC, A.add, MAGIC, A.not_equal)

    def firsts(b):
        for k in (2 * b, 2 * b + 1):
            mm(ps(FB, 256, 512), R("tri", 128 * k, 128 * k + 128), mk("ff", k), False, k == NK - 1)
            if k < NK - 1:
                mm(ps(FB, 256, 512), power(6 - k), R("nmag"), False, False)

    def counts(h):
        tolist(ps(4 + h, 0, 64), "ff", 1024 * h, 1024 * h + 1024, "bigc", first=False)

    def thresholds(t):
        return [lambda k=k: act(mk("th", k), mk(nbuf[t % 2], k), FN.Identity, scale=1.125 * 2 ** (8 - k) / OFF, bias=-2.0 ** (5 - k))
                for k in range(NK)]

    ts(R("n0"), R("mini"), -OFF, A.mult, OFF, A.add)
    for j in range(2):
        ts(R("uv", 8 * j, 8 * j + 8), R("sel", 16, 144, 16), col("wts", j), A.mult)
    for k in sorted(range(NK), key=lambda k: k // 2 not in SM):
        if k // 2 in SM:
            ts(mk("mz", k), R("zb0"), col("mini", k), A.mult)
        else:
            ts(mk("mz", k), R("zb0"), col("n0", k), A.max)
    ts(R("nuv"), R("uv"), -1.0, A.mult)
    before_sums()
    sums()
    for k in range(NK):
        if k // 2 in SG:
            act(mk("na", k), R("ones", 0, 256), FN.Identity, scale=col("n0", k))
    merge(constants_sum, [lambda k=k: ts(mk("na", k), R("ones", 0, 256), col("n0", k), A.mult) for k in range(NK) if k // 2 not in SG])
    merge([thresholds(0)[k] for k in range(NK) if k // 2 in SG])
    mm(ps(6, 0, 256), R("ident"), R("zb0"), True, True)
    for b in range(4):
        before_probe(0, b)
    before_none(0)
    before_firsts()
    merge(constants_key[0::2], places, constants_key[1::2])
    before_count(0)
    before_count(1)

    late = [constants_write[:6], constants_write[6:10], [thresholds(0)[k] for k in range(NK) if k // 2 not in SG],
            turns[:3], turns[3:6], constants_write[10:], turns[6:10], turns[10:13], turns[13:]]

    for t in range(STEPS):
        last = t == STEPS - 1
        cur, nxt, z, zn, nz = nbuf[t % 2], nbuf[(t + 1) % 2], R("zb%d" % t), "zb%d" % (t + 1), R("nz%d" % t)

        def moved(lo, hi):
            return G(R(cur), R("mvu", 16 * lo - 16, 16 * hi - 16))

        def none():
            mm(ps(7, 0, 256), R("nhalf"), mk("xy", 0), False, False)
            mm(ps(7, 0, 256), R("magic"), R("ones", 0, 256), False, True)

        def send():
            act(nz, R("dz"), FN.Abs)
            if not last:
                rid, pid = topo.addr(nxt_core, core)
                hold("G", [nz], [])
                g.remote_dma(out_ap=ap(R(zn)), in_ap=ap(nz), remote_sem=T.sem["arr%d" % (t + 1)], local_sem=T.sem["sent"],
                             pid=pid, routing_id=rid, dma_engine_mask=topo.mask(core, nxt_core))
                note("arr%d" % (t + 1), len(topo.engines(prv_core, core)), [], [R(zn)])
            store(T["yz"][:, NP * t:NP * t + NP], nz)

        def move(i):
            lo, hi = MOVES[i]
            if i in VMOVE:
                cp(R(nxt, 256 * lo, 256 * hi), moved(lo, hi))
            else:
                act(R(nxt, 256 * lo, 256 * hi), moved(lo, hi), FN.Copy)

        def others():
            for d in range(16):
                mm(ps(7, d, WD, 16), R("rot", 128 * d, 128 * d + 128), R("hx", 0, NPAIR), False, False)

        def own():
            for d in range(16):
                mm(ps(7, d, WD, 16), R("nid"), R("hx", 32, 32 + NPAIR), False, d == 15)

        def header(b):
            for h in range(2):
                mm(ps(b, 256 * h, 256 * h + 256), R("ident"), R(zn), False, h == 1)

        def part(name, h):
            return R(name, CUT, WD) if h else R(name, 0, CUT)

        def scan(h):
            op("V", V.tensor_tensor_scan, ["out"], out=part("st", h), data0=part("eq", h), data1=part("clamp", h), initial=0.0,
               op0=A.min, op1=A.max)

        def scatter(m):
            blk = BLOCKS[m]
            cp(G(R("tab"), R("scu", 4 * m, 4 * m + len(blk))), R("zb%d" % t, 16 * blk[0], 16 * blk[-1] + 16))

        def result(i):
            lo, hi = ((1, 3), (3, 5), (5, 7), (7, 8))[i]
            if i % 2 == 0:
                act(R("mo", 256 * lo, 256 * hi), moved(lo, hi), FN.Relu, scale=-1.0, bias=ONE)
            else:
                ts(R("mo", 256 * lo, 256 * hi), moved(lo, hi), 1.0, A.is_lt)
            store(T["ym"][:, 256 * lo:256 * hi], R("mo", 256 * lo, 256 * hi))

        parity = [lambda: act(R("par"), ps(4, 0, 16), FN.Identity, scale=0.5, bias=M64, accum_out=col("px", 0)),
                  lambda: act(col("px", 1), col("px", 0), FN.Identity, bias=PMAGIC),
                  lambda: act(col("px", 2), col("px", 1), FN.Identity, bias=NMAGIC),
                  lambda: act(col("px", 3), col("px", 2), FN.Identity, scale=-1.0, bias=col("px", 0)),
                  lambda: act(R("lim"), R("c128", 0, 64), FN.Identity, scale=col("px", 3), bias=112.0)]
        numbered = {
            "g": lambda b: gather(t, b), "d": lambda b: difference(t, b), "f": failing, "r": firsts, "c": counts,
            "y": lambda h: tt(R("ky", 64 * h, 64 * h + 64), R("base", 64 * h, 64 * h + 64), ps(4 + h, 0, 64), A.max),
            "k": lambda h: tt(R("kc" if h else "ka"), R("ky", 64 * h, 64 * h + 32), R("ky", 64 * h + 32, 64 * h + 64), A.min),
            "m": move, "p": lambda i: parity[i](), "w": lambda i: written()[i](), "z": header,
            "n": lambda b: mm(ps(b), R("neg"), bk(nxt, b), True, False),
            "x": lambda b: act(bk("mz", b), ps(b), FN.Relu),
            "v": lambda k: tt(mk("mz", k), mk(nxt, k), ps(6, 0, 256), A.max),
            "e": lambda h: act(part("eq", h), part("ps7", h), FN.Abs, scale=4 * TOP), "a": scan,
            "u": lambda h: ts(R("scu", 16 * h, 16 * h + 16), G(part("st", h), col("lst", 6 + 2 * h)), -1.0, A.mult, TOP, A.add),
            "s": scatter, "h": lambda i: places[i](), "t": lambda k: thresholds(t + 1)[k](),
            "b": lambda b: before_probe(t + 1, b), "l": before_count, "o": result,
            "q": lambda i: merge(late[i] if t == 0 else [])}
        named = {
            "none": none, "ncol": lambda: act(R("tab", NW, NW + NP), ps(7, 0, 256), FN.Identity, bias=NMAGIC),
            "kb": lambda: tt(R("kb"), R("ka"), R("none"), A.min),
            "kd": lambda: tt(R("kd"), R("kc"), R("kb"), A.min),
            "key": lambda: tt(R("key"), R("kd", 0, 16), R("kd", 16, 32), A.min),
            "ssb": lambda: act(R("ssb"), ps(FB, 256, 512), FN.Identity, scale=-1.0, bias=PMAGIC),
            "hs": lambda: ts(R("hs"), R("key"), 8191, A.bitwise_and),
            "ju": lambda: ts(R("ju"), R("key"), 1.0 / 8192, A.mult, 1024.0, A.add),
            "hsu": lambda: cp(R("hsu"), R("hs")),
            "ge": lambda: tt(R("ge"), G(R("key"), R("lrep")), R("kge"), A.is_lt),
            "dz": lambda: tt(R("dz"), G(R("tab"), R("hsu")), z, A.subtract), "send": send,
            "stay": lambda: mm(ps(7, 0, 112), R("ident"), R("jc", 0, 112), True, False),
            "down": lambda: mm(ps(7, 0, 112), power(8), R("ge", 0, 112), False, True),
            "mvu": lambda: ts(R("mvu"), ps(7, 0, 112), col("qf", 0), A.add),
            "ub": lambda: tt(R("ub"), G(R("th"), R("ju")), R("ssb"), A.is_le),
            "uz": lambda: tt(R("uz"), R("ub"), ps(6, 0, 256), A.mult),
            "su": lambda: tolist(ps(5, 0, 16), "uz", 0, 256, "bigu"), "sv": lambda: tolist(ps(5, 16, 32), "uz", 0, 256, "bigv"),
            "nm": lambda: mm(ps(4, 0, 16), R("ones", 0, 128), R("ge", 112, 128), True, True),
            "code": lambda: act(mk(nxt, 0), R("ub"), FN.Identity, scale=-OFF, bias=POFF),
            "inval": lambda: mm(ps(7, 0, WD), R("ident"), R("inval"), True, False),
            "hx": lambda: ts(R("hx"), G(R("pl"), R("lst", 0, 4)), -2048.0, A.add),
            "npl": lambda: ts(R("npl"), R("pl"), -1.0, A.mult, TOP, A.add),
            "slot": lambda: cp(G(R("clamp"), col("lst", 4)), R("npl")),
            "others": others, "own": own, "zps": lambda: mm(ps(6, 0, 256), R("ident"), R(zn), True, True),
            "presum": before_sums, "sums": sums, "prenone": lambda: before_none(t + 1), "prefirst": before_firsts,
            "out": lambda: store(T["ym"][:, 0:256], R("ub"))}
        for name in (PROBE + " " + (LAST if last else WRITE)).split():
            if name in named:
                named[name]()
            else:
                numbered[name[0]](int(name[1]))
    g.sync.wait_ge(T.sem["outs"], stored[0])
    for e in QUEUES:
        g.sync.wait_ge(T.sem[semof[e]], count[e])
    g.wait_ge(T.sem["sent"], (STEPS - 1) * len(topo.engines(core, nxt_core)))
